import numpy as np
import ml_dtypes


def mxq(x, axis, fmt="e4m3"):
    dtype, down = {"e4m3": (ml_dtypes.float8_e4m3fn, 7), "e5m2": (ml_dtypes.float8_e5m2, 14)}[fmt]
    v = np.moveaxis(np.asarray(x, np.float32).astype(ml_dtypes.bfloat16).astype(np.float64), axis, -1)
    blocks = v.reshape(v.shape[:-1] + (-1, 32))
    amax = np.abs(blocks).max(-1, keepdims=True)
    byte = np.maximum(np.where(amax > 0, np.frexp(amax)[1] - 1 + 127, 0) - down, 1)
    scale = np.exp2(byte - 127.0)
    codes = (blocks / scale).astype(np.float32).astype(dtype).astype(np.float64)
    return np.moveaxis((codes * scale).reshape(v.shape), -1, axis)


WIDE = False


def mx_kscale(k):
    if not WIDE:
        return np.ones(k)
    levels = np.array([10, -10, 5, -5, 0])
    if k % 512:
        return np.exp2(np.random.permutation(np.resize(levels, k // 32))).repeat(32)
    a = np.empty((k // 512, 16))
    for p in range(k // 512):
        a[p, :8] = np.random.permutation(np.resize(levels, 8))
        for g in range(8):
            far = levels[np.abs(levels - a[p, g]) >= 10]
            a[p, g + 8] = far[np.random.randint(len(far))]
    return np.exp2(a.ravel()).repeat(32)


def f64(x):
    return np.asarray(x).astype(np.float64)


def striped(idx):
    return np.tile(idx.reshape(-1, 16).T, (8, 1)).astype(np.uint16)


def unstriped(offs):
    return offs[:16].T.reshape(-1).astype(np.int64)


def pack_weight(w):
    k, n = w.shape
    w = f64(np.asarray(w, np.float32).astype(ml_dtypes.bfloat16)).reshape(k // 32, 32, n)
    amax = np.abs(w).max(1)
    byte = np.clip(np.where(amax > 0, np.frexp(amax)[1] - 1 + 127 - 7, 1), 1, 254)
    scaled = (w * np.exp2(127.0 - byte)[:, None, :]).reshape(k, n).astype(np.float32)
    words = np.ascontiguousarray(scaled.reshape(k // 512, 128, 4, n).transpose(0, 1, 3, 2)).astype(ml_dtypes.float8_e4m3fn).view(np.uint8)
    return words, np.ascontiguousarray(byte.astype(np.uint8).reshape(k // 512, 16, n))


def unpack_weight(words, scales):
    g, p, n, _ = words.shape
    vals = np.ascontiguousarray(words).view(ml_dtypes.float8_e4m3fn).astype(np.float64) * np.repeat(np.exp2(scales.astype(np.float64) - 127.0), 8, axis=1)[..., None]
    return vals.transpose(0, 1, 3, 2).reshape(g * 512, n)


E2M1 = np.array([0.0, 0.5, 1.0, 1.5, 2.0, 3.0, 4.0, 6.0, -0.0, -0.5, -1.0, -1.5, -2.0, -3.0, -4.0, -6.0])


def pack_fp4(w):
    k, n = w.shape
    w = f64(np.asarray(w, np.float32).astype(ml_dtypes.bfloat16)).reshape(k // 32, 32, n)
    amax = np.abs(w).max(1)
    mant, ex = np.frexp(amax / 6.0)
    byte = np.clip(np.where(amax > 0, np.where(mant > 0.5, ex, ex - 1) + 127, 1), 1, 254)
    scaled = (w * np.exp2(127.0 - byte)[:, None, :]).reshape(k, n).astype(np.float32)
    c = np.ascontiguousarray(scaled.reshape(k // 512, 128, 4, n).transpose(0, 1, 3, 2)).astype(ml_dtypes.float4_e2m1fn).view(np.uint8) & 0xF
    words = (c[..., 0::2] | (c[..., 1::2] << 4)).reshape(k // 512, 128, 2 * n)
    return np.ascontiguousarray(words), np.ascontiguousarray(byte.astype(np.uint8).reshape(k // 512, 16, n))


def unpack_fp4(words, scales):
    g, _, n = scales.shape
    words = np.ascontiguousarray(words).reshape(g, 128, n, 2)
    nib = np.empty((g, 128, n, 4), np.uint8)
    nib[..., 0::2] = words & 0xF
    nib[..., 1::2] = words >> 4
    vals = E2M1[nib] * np.repeat(np.exp2(scales.astype(np.float64) - 127.0), 8, axis=1)[..., None]
    return vals.transpose(0, 1, 3, 2).reshape(g * 512, n)


def relu(v):
    return np.maximum(v, 0.0)


K, T, S, H, N, U = 1024, 2048, 1024, 512, 256, 2048
P = 2 ** 7


def setup_inputs():
    n = np.random.standard_normal
    s = mx_kscale(K)[:, None]
    u = mx_kscale(H)
    packed_xT = pack_weight(n((K, T)) * s)
    packed_w2 = pack_fp4(n((H, N)) / np.sqrt(H) / u[:, None])
    return {
        "x_words": packed_xT[0],
        "x_scales": packed_xT[1],
        "gate": np.tile(np.random.uniform(0.5, 1.5, S), (P, 1)).astype(np.float32),
        "w1": (n((K, H)) / np.sqrt(K) / s * u).astype(np.float32),
        "w2_words": packed_w2[0],
        "w2_scales": packed_w2[1],
        "offs": striped(np.random.permutation(T)[:S]),
        "dst": striped(np.random.permutation(U)[:S]),
    }


def reference(x_words, x_scales, gate, w1, w2_words, w2_scales, offs, dst):
    xq = unpack_weight(x_words, x_scales)[:, unstriped(offs)]
    h = relu(mxq(f64(w1), 0, "e4m3").T @ xq)
    y = unpack_fp4(w2_words, w2_scales).T @ mxq(h, 0, "e4m3")
    out = np.zeros((N, U))
    out[:, unstriped(dst)] = y * f64(gate)[:1]
    return out

@@ -1,0 +1,172 @@
+from contextlib import ExitStack
+
+import concourse.mybir as mybir
+
+F32 = mybir.dt.float32
+BF16 = mybir.dt.bfloat16
+I32 = mybir.dt.int32
+U32 = mybir.dt.uint32
+U16 = mybir.dt.uint16
+U8 = mybir.dt.uint8
+FP8X4 = mybir.dt.float8_e4m3fn_x4
+FP4X4 = mybir.dt.float4_e2m1fn_x4
+RELU = mybir.ActivationFunctionType.Relu
+COPY = mybir.ActivationFunctionType.Copy
+MULT = mybir.AluOpType.mult
+
+K, T, S, H, N, U = 1024, 2048, 1024, 512, 256, 2048
+P = 128
+FLOPS = 2 * K * H * S + 2 * H * N * S
+LEAD = 256
+
+
+def tile_picked_route2_mlprelu_p_kernel(tc, x_words, x_scales, gate, w1, w2_words, w2_scales, offs, dst, out):
+    nc = tc.nc
+    with ExitStack() as ctx:
+        lists = ctx.enter_context(tc.tile_pool(name="lists", bufs=1))
+        keep = ctx.enter_context(tc.tile_pool(name="keep", bufs=1))
+        shared = ctx.enter_context(tc.tile_pool(name="shared", bufs=1))
+        psum = ctx.enter_context(tc.psum_pool(name="psum", bufs=1))
+
+        def sb(name, shape, dtype, tag=None):
+            return keep.tile(shape, dtype, name=name, tag=tag or name, align_bytes=64)
+
+        def at(offset, name, shape, dtype):
+            return shared.tile(shape, dtype, name=name, offset=offset, align_bytes=64)
+
+        RAW = (0, 8192)
+        XS = 16384
+        STAGE = {(1, 1): XS + 1024, (0, 0): XS + 3072, (0, 1): XS + 5120, (1, 0): XS + 7168}
+
+        def bank(name, b, shape):
+            return psum.tile(shape, F32, name=name, tag="bank%d" % b)
+
+        offs_sb = lists.tile([P, S // 16], U16, name="offs_sb")
+        dst_sb = lists.tile([P, S // 16], U16, name="dst_sb")
+        nc.sync.dma_start(offs_sb[:], offs)
+        nc.sync.dma_start(dst_sb[:], dst)
+
+        xs_all = at(XS, "xs_all", [P, T], U8)
+        nc.vector.memset(xs_all[:].bitcast(I32), 0)
+        for q in range(4):
+            nc.scalar.dma_start(xs_all[32 * q : 32 * q + 8, :].bitcast(I32), x_scales[:, 4 * q : 4 * q + 4, :].bitcast(I32))
+
+        w1_raw = []
+        for z in range(2):
+            raw = at(RAW[z], "w1_raw%d" % z, [P, 4, H], F32)
+            nc.sync.dma_start(raw[:], w1[512 * z : 512 * (z + 1), :].rearrange("(p j) c -> p j c", j=4))
+            w1_raw.append(raw)
+        xw_all = []
+        for z in range(2):
+            xw = sb("xw_all%d" % z, [P, T], I32)
+            nc.sync.dma_start(xw[:], x_words[z].rearrange("p c r -> p (c r)").bitcast(I32))
+            xw_all.append(xw)
+
+        zero = sb("zero", [P, 1], F32)
+        nc.vector.memset(zero[:], 0.0)
+        win = [sb("win%d" % b, [P, U], F32) for b in range(2)]
+        nc.scalar.activation(out=win[1][:, :LEAD], in_=zero[:].to_broadcast([P, LEAD]), func=COPY)
+        nc.vector.memset(win[0][:], 0.0)
+        nc.vector.memset(win[1][:, LEAD:], 0.0)
+
+        def entries(lst, a, b):
+            return lst[:, a // 16 : b // 16]
+
+        def gather(picked, window, a, b):
+            nc.vector.tensor_copy(picked[:], window.indirect(entries(offs_sb, a, b)))
+            return picked
+
+        xs = {}
+        for a, b in ((0, 512), (512, 1024)):
+            xs[a] = gather(sb("xs%d" % a, [P, b - a], U8), xs_all[:], a, b)
+
+        w1c, w1s = {}, {}
+        staged = {}
+
+        def cast(z, u, copy):
+            staged[z, u] = at(STAGE[z, u], "w1_bf%d%d" % (z, u), [P, 2, P, 4], BF16)
+            copy(staged[z, u][:].rearrange("p t m j -> p m j t"),
+                 w1_raw[z][:].rearrange("p j (m t) -> p m j t", t=4)[:, :, :, 2 * u : 2 * u + 2])
+
+        def quant_w1(z, u):
+            w1c[z, u] = sb("w1c%d%d" % (z, u), [P, 2 * P], U32)
+            w1s[z, u] = at(XS + 256 * (2 * z + u), "w1s%d%d" % (z, u), [P, 2 * P], U8)
+            nc.vector.quantize_mx(out=w1c[z, u][:].bitcast(FP8X4), scales=w1s[z, u][:],
+                                  in_=staged[z, u][:].rearrange("p t m j -> p (t m j)"))
+
+        cast(0, 0, nc.scalar.copy)
+        cast(0, 1, nc.scalar.copy)
+        cast(1, 0, nc.scalar.copy)
+        quant_w1(0, 0)
+        cast(1, 1, nc.vector.tensor_copy)
+        quant_w1(0, 1)
+        quant_w1(1, 1)
+        quant_w1(1, 0)
+
+        gate_sb = at(RAW[0], "gate_sb", [P, S], F32)
+        w2w = at(RAW[1], "w2w", [P, 2 * N], U8)
+        w2s = at(RAW[1] + 2 * N, "w2s", [P, N], U8)
+        nc.sync.dma_start(gate_sb[:], gate)
+        nc.sync.dma_start(w2w[:].bitcast(I32), w2_words[0].bitcast(I32))
+        nc.vector.memset(w2s[:].bitcast(I32), 0)
+        for q in range(4):
+            nc.sync.dma_start(w2s[32 * q : 32 * q + 4, :].bitcast(I32), w2_scales[0, 4 * q : 4 * q + 4, :].bitcast(I32))
+
+        xw = {}
+        for z, a, b, offset in ((0, 0, 512, STAGE[0, 0]), (0, 512, 1024, STAGE[0, 1]), (1, 0, 256, STAGE[1, 1]),
+                                (1, 256, 512, STAGE[1, 1] + 1024), (1, 512, 1024, STAGE[1, 0])):
+            picked = gather(at(offset, "xw%d_%d" % (z, a), [P, b - a], U32), xw_all[z][:].bitcast(U32), a, b)
+            for c in range(a, b, P):
+                xw[z, c] = picked[:, c - a : c - a + P]
+
+        chunks = ((0, 256), (256, 512), (512, 1024))
+        hb = {a: sb("hb%d" % a, [P, b - a, 4], BF16) for a, b in chunks}
+        hc = {a: sb("hc%d" % a, [P, b - a], U32) for a, b in chunks}
+        hs = {a: sb("hs%d" % a, [P, b - a], U8) for a, b in chunks}
+
+        def hidden(c, b, a):
+            acc = bank("h%d" % c, b, [P, 4, P])
+            half = 512 * (c // 512)
+            for t in range(4):
+                cols = slice((t % 2) * P, (t % 2 + 1) * P)
+                for z in range(2):
+                    nc.tensor.matmul_mx(out=acc[:, t, :], lhsT=w1c[z, t // 2][:, cols].bitcast(FP8X4), lhsT_scale=w1s[z, t // 2][:, cols],
+                                        rhs=xw[z, c].bitcast(FP8X4), rhs_scale=xs[half][4 * z :, c - half : c - half + P],
+                                        start=(z == 0), stop=(z == 1))
+            nc.scalar.activation(out=hb[a][:, c - a : c - a + P, :], in_=acc[:].rearrange("p t n -> p n t"), func=RELU)
+
+        def quant(a, lo, hi):
+            nc.vector.quantize_mx(out=hc[a][:, lo - a : hi - a].bitcast(FP8X4), scales=hs[a][:, lo - a : hi - a],
+                                  in_=hb[a][:, lo - a : hi - a, :].rearrange("p n t -> p (n t)"))
+
+        def result(r, a, e, b):
+            acc = bank("y%d_%d" % (r, a), b, [P, e - a])
+            nc.tensor.matmul_mx(out=acc[:], lhsT=w2w[:, 2 * P * r : 2 * P * (r + 1)].bitcast(FP4X4), lhsT_scale=w2s[:, P * r : P * (r + 1)],
+                                rhs=hc[a][:].bitcast(FP8X4), rhs_scale=hs[a][:], start=True, stop=True)
+            y = sb("y%d_%d" % (r, a), [P, e - a], F32)
+            nc.scalar.copy(y[:], acc[:])
+            return y
+
+        def put(r, a, e, y):
+            nc.vector.tensor_tensor(win[r][:].indirect(entries(dst_sb, a, e)), y[:], gate_sb[:, a:e], MULT)
+
+        hidden(0, 0, 0)
+        quant(0, 0, 128)
+        hidden(128, 1, 0)
+        quant(0, 128, 256)
+        hidden(256, 2, 256)
+        put(0, 0, 256, result(0, 0, 256, 0))
+        hidden(384, 2, 256)
+        quant(256, 256, 512)
+        put(1, 0, 256, result(1, 0, 256, 2))
+        hidden(512, 0, 512)
+        put(0, 256, 512, result(0, 256, 512, 1))
+        hidden(640, 2, 512)
+        hidden(768, 0, 512)
+        hidden(896, 2, 512)
+        quant(512, 512, 1024)
+        put(1, 256, 512, result(1, 256, 512, 2))
+        put(0, 512, 1024, result(0, 512, 1024, 0))
+        nc.sync.dma_start(out[0:P, :], win[0][:])
+        put(1, 512, 1024, result(1, 512, 1024, 1))
+        nc.sync.dma_start(out[P : 2 * P, :], win[1][:])

@@ -17,7 +17,7 @@ MULT = mybir.AluOpType.mult
 K, T, S, H, N, U = 1024, 2048, 1024, 512, 256, 2048
 P = 128
 FLOPS = 2 * K * H * S + 2 * H * N * S
-LEAD = 256
+LEAD = 96
 
 
 def tile_picked_route2_mlprelu_p_kernel(tc, x_words, x_scales, gate, w1, w2_words, w2_scales, offs, dst, out):
@@ -35,11 +35,14 @@ def tile_picked_route2_mlprelu_p_kernel(tc, x_words, x_scales, gate, w1, w2_word
             return shared.tile(shape, dtype, name=name, offset=offset, align_bytes=64)
 
         RAW = (0, 8192)
-        XS = 16384
-        STAGE = {(1, 1): XS + 1024, (0, 0): XS + 3072, (0, 1): XS + 5120, (1, 0): XS + 7168}
+        XS = 16384 + 1984
+        STAGE = {(0, 1): 16384, (1, 1): XS + 1984, (0, 0): XS + 4032, (1, 0): XS + 6080}
+        HB0 = XS + 8128
+        XW = (HB0 + 2048, HB0 + 2048 + 8192 + N)
+        W2S = XW[0] + 8192
 
         def bank(name, b, shape):
-            return psum.tile(shape, F32, name=name, tag="bank%d" % b)
+            return psum.tile(shape, F32, name=name, offset=2048 * b)
 
         offs_sb = lists.tile([P, S // 16], U16, name="offs_sb")
         dst_sb = lists.tile([P, S // 16], U16, name="dst_sb")
@@ -56,18 +59,22 @@ def tile_picked_route2_mlprelu_p_kernel(tc, x_words, x_scales, gate, w1, w2_word
             raw = at(RAW[z], "w1_raw%d" % z, [P, 4, H], F32)
             nc.sync.dma_start(raw[:], w1[512 * z : 512 * (z + 1), :].rearrange("(p j) c -> p j c", j=4))
             w1_raw.append(raw)
-        xw_all = []
-        for z in range(2):
-            xw = sb("xw_all%d" % z, [P, T], I32)
-            nc.sync.dma_start(xw[:], x_words[z].rearrange("p c r -> p (c r)").bitcast(I32))
-            xw_all.append(xw)
-
-        zero = sb("zero", [P, 1], F32)
+        zero = at(W2S - 64, "zero", [P, LEAD], F32)
         nc.vector.memset(zero[:], 0.0)
         win = [sb("win%d" % b, [P, U], F32) for b in range(2)]
-        nc.scalar.activation(out=win[1][:, :LEAD], in_=zero[:].to_broadcast([P, LEAD]), func=COPY)
-        nc.vector.memset(win[0][:], 0.0)
-        nc.vector.memset(win[1][:, LEAD:], 0.0)
+        nc.scalar.activation(out=win[1][:, :LEAD], in_=zero[:], func=COPY)
+        nc.vector.memset(win[0][:].bitcast(I32), 0)
+        nc.vector.memset(win[1][:, LEAD:].bitcast(I32), 0)
+
+        xw_all = []
+        for z in range(2):
+            xw = at(XW[z], "xw_all%d" % z, [P, T], I32)
+            nc.sync.dma_start(xw[:], x_words[z].rearrange("p c r -> p (c r)").bitcast(I32))
+            xw_all.append(xw)
+        w2s = at(W2S, "w2s", [P, N], U8)
+        nc.gpsimd.memset(w2s[:].bitcast(I32), 0)
+        for q in range(4):
+            nc.sync.dma_start(w2s[32 * q : 32 * q + 4, :].bitcast(I32), w2_scales[0, 4 * q : 4 * q + 4, :].bitcast(I32))
 
         def entries(lst, a, b):
             return lst[:, a // 16 : b // 16]
@@ -85,42 +92,44 @@ def tile_picked_route2_mlprelu_p_kernel(tc, x_words, x_scales, gate, w1, w2_word
 
         def cast(z, u, copy):
             staged[z, u] = at(STAGE[z, u], "w1_bf%d%d" % (z, u), [P, 2, P, 4], BF16)
-            copy(staged[z, u][:].rearrange("p t m j -> p m j t"),
-                 w1_raw[z][:].rearrange("p j (m t) -> p m j t", t=4)[:, :, :, 2 * u : 2 * u + 2])
+            copy(staged[z, u][:].rearrange("p t m j -> p m t j"),
+                 w1_raw[z][:].rearrange("p j (m t) -> p m t j", t=4)[:, :, 2 * u : 2 * u + 2, :])
 
         def quant_w1(z, u):
             w1c[z, u] = sb("w1c%d%d" % (z, u), [P, 2 * P], U32)
-            w1s[z, u] = at(XS + 256 * (2 * z + u), "w1s%d%d" % (z, u), [P, 2 * P], U8)
+            w1s[z, u] = at(XS + 128 + 256 * (2 * z + u), "w1s%d%d" % (z, u), [P, 2 * P], U8)
             nc.vector.quantize_mx(out=w1c[z, u][:].bitcast(FP8X4), scales=w1s[z, u][:],
                                   in_=staged[z, u][:].rearrange("p t m j -> p (t m j)"))
 
         cast(0, 0, nc.scalar.copy)
-        cast(0, 1, nc.scalar.copy)
         cast(1, 0, nc.scalar.copy)
+        cast(0, 1, nc.vector.tensor_copy)
         quant_w1(0, 0)
-        cast(1, 1, nc.vector.tensor_copy)
         quant_w1(0, 1)
+        cast(1, 1, nc.vector.tensor_copy)
         quant_w1(1, 1)
         quant_w1(1, 0)
 
         gate_sb = at(RAW[0], "gate_sb", [P, S], F32)
-        w2w = at(RAW[1], "w2w", [P, 2 * N], U8)
-        w2s = at(RAW[1] + 2 * N, "w2s", [P, N], U8)
-        nc.sync.dma_start(gate_sb[:], gate)
+        w2w = at(RAW[0] + 4 * S, "w2w", [P, 2 * N], U8)
         nc.sync.dma_start(w2w[:].bitcast(I32), w2_words[0].bitcast(I32))
-        nc.vector.memset(w2s[:].bitcast(I32), 0)
-        for q in range(4):
-            nc.sync.dma_start(w2s[32 * q : 32 * q + 4, :].bitcast(I32), w2_scales[0, 4 * q : 4 * q + 4, :].bitcast(I32))
+        nc.sync.dma_start(gate_sb[:], gate)
 
         xw = {}
-        for z, a, b, offset in ((0, 0, 512, STAGE[0, 0]), (0, 512, 1024, STAGE[0, 1]), (1, 0, 256, STAGE[1, 1]),
-                                (1, 256, 512, STAGE[1, 1] + 1024), (1, 512, 1024, STAGE[1, 0])):
+
+        def pick(z, a, b, offset):
             picked = gather(at(offset, "xw%d_%d" % (z, a), [P, b - a], U32), xw_all[z][:].bitcast(U32), a, b)
             for c in range(a, b, P):
                 xw[z, c] = picked[:, c - a : c - a + P]
 
+        pick(0, 0, 512, STAGE[0, 0])
+        pick(1, 0, 256, STAGE[1, 1])
+        pick(1, 256, 512, STAGE[1, 1] + 1024)
+        pick(0, 512, 1024, STAGE[1, 0])
+
         chunks = ((0, 256), (256, 512), (512, 1024))
-        hb = {a: sb("hb%d" % a, [P, b - a, 4], BF16) for a, b in chunks}
+        hb = {0: sb("hb0", [P, P, 4], BF16), 128: at(HB0, "hb128", [P, P, 4], BF16),
+              256: at(STAGE[0, 1], "hb256", [P, 256, 4], BF16), 512: sb("hb512", [P, 512, 4], BF16)}
         hc = {a: sb("hc%d" % a, [P, b - a], U32) for a, b in chunks}
         hs = {a: sb("hs%d" % a, [P, b - a], U8) for a, b in chunks}
 
@@ -137,14 +146,14 @@ def tile_picked_route2_mlprelu_p_kernel(tc, x_words, x_scales, gate, w1, w2_word
 
         def quant(a, lo, hi):
             nc.vector.quantize_mx(out=hc[a][:, lo - a : hi - a].bitcast(FP8X4), scales=hs[a][:, lo - a : hi - a],
-                                  in_=hb[a][:, lo - a : hi - a, :].rearrange("p n t -> p (n t)"))
+                                  in_=hb[lo][:].rearrange("p n t -> p (n t)"))
 
-        def result(r, a, e, b):
-            acc = bank("y%d_%d" % (r, a), b, [P, e - a])
-            nc.tensor.matmul_mx(out=acc[:], lhsT=w2w[:, 2 * P * r : 2 * P * (r + 1)].bitcast(FP4X4), lhsT_scale=w2s[:, P * r : P * (r + 1)],
+        def result(r, a, e, b, banks=1):
+            acc = bank("y%d_%d" % (r, a), b, [P, 512 * banks])[:, : e - a]
+            nc.tensor.matmul_mx(out=acc, lhsT=w2w[:, 2 * P * r : 2 * P * (r + 1)].bitcast(FP4X4), lhsT_scale=w2s[:, P * r : P * (r + 1)],
                                 rhs=hc[a][:].bitcast(FP8X4), rhs_scale=hs[a][:], start=True, stop=True)
             y = sb("y%d_%d" % (r, a), [P, e - a], F32)
-            nc.scalar.copy(y[:], acc[:])
+            nc.scalar.copy(y[:], acc)
             return y
 
         def put(r, a, e, y):
@@ -152,21 +161,24 @@ def tile_picked_route2_mlprelu_p_kernel(tc, x_words, x_scales, gate, w1, w2_word
 
         hidden(0, 0, 0)
         quant(0, 0, 128)
-        hidden(128, 1, 0)
+        hidden(128, 3, 128)
         quant(0, 128, 256)
-        hidden(256, 2, 256)
-        put(0, 0, 256, result(0, 0, 256, 0))
-        hidden(384, 2, 256)
+        pick(1, 512, 768, HB0)
+        hidden(256, 4, 256)
+        y00 = result(0, 0, 256, 0, banks=3)
+        put(0, 0, 256, y00)
+        hidden(384, 0, 256)
         quant(256, 256, 512)
-        put(1, 0, 256, result(1, 0, 256, 2))
-        hidden(512, 0, 512)
-        put(0, 256, 512, result(0, 256, 512, 1))
+        pick(1, 768, 1024, STAGE[0, 1])
+        put(1, 0, 256, result(1, 0, 256, 0))
+        put(0, 256, 512, result(0, 256, 512, 3))
+        hidden(512, 1, 512)
         hidden(640, 2, 512)
-        hidden(768, 0, 512)
-        hidden(896, 2, 512)
+        hidden(768, 5, 512)
+        hidden(896, 6, 512)
         quant(512, 512, 1024)
-        put(1, 256, 512, result(1, 256, 512, 2))
-        put(0, 512, 1024, result(0, 512, 1024, 0))
+        put(1, 256, 512, result(1, 256, 512, 6))
+        put(0, 512, 1024, result(0, 512, 1024, 4))
         nc.sync.dma_start(out[0:P, :], win[0][:])
-        put(1, 512, 1024, result(1, 512, 1024, 1))
+        put(1, 512, 1024, result(1, 512, 1024, 7))
         nc.sync.dma_start(out[P : 2 * P, :], win[1][:])

@@ -28,49 +28,52 @@ def tile_picked_route2_mlprelu_p_kernel(tc, x_words, x_scales, gate, w1, w2_word
         shared = ctx.enter_context(tc.tile_pool(name="shared", bufs=1))
         psum = ctx.enter_context(tc.psum_pool(name="psum", bufs=1))
 
-        def sb(name, shape, dtype, tag=None):
-            return keep.tile(shape, dtype, name=name, tag=tag or name, align_bytes=64)
+        def sb(name, shape, dtype):
+            return keep.tile(shape, dtype, name=name, align_bytes=64)
 
         def at(offset, name, shape, dtype):
             return shared.tile(shape, dtype, name=name, offset=offset, align_bytes=64)
 
-        RAW = (0, 8192)
-        XS = 16384 + 1984
-        STAGE = {(0, 1): 16384, (1, 1): XS + 1984, (0, 0): XS + 4032, (1, 0): XS + 6080}
-        HB0 = XS + 8128
-        XW = (HB0 + 2048, HB0 + 2048 + 8192 + N)
-        W2S = XW[0] + 8192
-
         def bank(name, b, shape):
             return psum.tile(shape, F32, name=name, offset=2048 * b)
+
+        RAW = (0, 16384)
+        XW = (8192, 24576 + N)
+        W2S = 24576
 
         offs_sb = lists.tile([P, S // 16], U16, name="offs_sb")
         dst_sb = lists.tile([P, S // 16], U16, name="dst_sb")
         nc.sync.dma_start(offs_sb[:], offs)
+        w1_raw, xw_all = {}, {}
+
+        def load_w1(z):
+            w1_raw[z] = at(RAW[z], "w1_raw%d" % z, [P, 4, H], F32)
+            nc.sync.dma_start(w1_raw[z][:], w1[512 * z : 512 * (z + 1), :].rearrange("(p j) c -> p j c", j=4))
+
+        def load_x(z):
+            xw_all[z] = at(XW[z], "xw_all%d" % z, [P, T], I32)
+            nc.sync.dma_start(xw_all[z][:], x_words[z].rearrange("p c r -> p (c r)").bitcast(I32))
+
+        load_w1(0)
         nc.sync.dma_start(dst_sb[:], dst)
 
-        xs_all = at(XS, "xs_all", [P, T], U8)
+        xs_all = sb("xs_all", [P, T], U8)
         nc.vector.memset(xs_all[:].bitcast(I32), 0)
         for q in range(4):
             nc.scalar.dma_start(xs_all[32 * q : 32 * q + 8, :].bitcast(I32), x_scales[:, 4 * q : 4 * q + 4, :].bitcast(I32))
 
-        w1_raw = []
-        for z in range(2):
-            raw = at(RAW[z], "w1_raw%d" % z, [P, 4, H], F32)
-            nc.sync.dma_start(raw[:], w1[512 * z : 512 * (z + 1), :].rearrange("(p j) c -> p j c", j=4))
-            w1_raw.append(raw)
-        zero = at(W2S - 64, "zero", [P, LEAD], F32)
-        nc.vector.memset(zero[:], 0.0)
         win = [sb("win%d" % b, [P, U], F32) for b in range(2)]
-        nc.scalar.activation(out=win[1][:, :LEAD], in_=zero[:], func=COPY)
-        nc.vector.memset(win[0][:].bitcast(I32), 0)
-        nc.vector.memset(win[1][:, LEAD:].bitcast(I32), 0)
+        zero_v = at(RAW[1] - 64, "zero_v", [P, 32], F32)
+        zero_s = at(W2S + N - 64, "zero_s", [P, 32], F32)
+        nc.vector.memset(zero_v[:], 0.0)
+        nc.vector.memset(zero_s[:], 0.0)
+        nc.scalar.activation(out=win[1][:, :32], in_=zero_s[:], func=COPY)
+        nc.vector.tensor_copy(win[0][:].rearrange("p (a b) -> p a b", b=32), zero_v[:].unsqueeze(1).to_broadcast([P, U // 32, 32]))
+        nc.vector.tensor_copy(win[1][:, 32:], win[0][:, 32:])
 
-        xw_all = []
-        for z in range(2):
-            xw = at(XW[z], "xw_all%d" % z, [P, T], I32)
-            nc.sync.dma_start(xw[:], x_words[z].rearrange("p c r -> p (c r)").bitcast(I32))
-            xw_all.append(xw)
+        load_x(0)
+        load_w1(1)
+        load_x(1)
         w2s = at(W2S, "w2s", [P, N], U8)
         nc.gpsimd.memset(w2s[:].bitcast(I32), 0)
         for q in range(4):
@@ -79,33 +82,39 @@ def tile_picked_route2_mlprelu_p_kernel(tc, x_words, x_scales, gate, w1, w2_word
         def entries(lst, a, b):
             return lst[:, a // 16 : b // 16]
 
-        def gather(picked, window, a, b):
+        def gather(name, dtype, window, a, b):
+            picked = sb(name, [P, b - a], dtype)
             nc.vector.tensor_copy(picked[:], window.indirect(entries(offs_sb, a, b)))
             return picked
 
-        xs = {}
-        for a, b in ((0, 512), (512, 1024)):
-            xs[a] = gather(sb("xs%d" % a, [P, b - a], U8), xs_all[:], a, b)
+        xs = gather("xs", U8, xs_all[:], 0, S)
 
-        w1c, w1s = {}, {}
-        staged = {}
+        w1c, w1s, staged, xw = {}, {}, {}, {}
 
         def cast(z, u, copy):
-            staged[z, u] = at(STAGE[z, u], "w1_bf%d%d" % (z, u), [P, 2, P, 4], BF16)
+            staged[z, u] = sb("w1_bf%d%d" % (z, u), [P, 2, P, 4], BF16)
             copy(staged[z, u][:].rearrange("p t m j -> p m t j"),
                  w1_raw[z][:].rearrange("p j (m t) -> p m t j", t=4)[:, :, 2 * u : 2 * u + 2, :])
 
         def quant_w1(z, u):
             w1c[z, u] = sb("w1c%d%d" % (z, u), [P, 2 * P], U32)
-            w1s[z, u] = at(XS + 128 + 256 * (2 * z + u), "w1s%d%d" % (z, u), [P, 2 * P], U8)
+            w1s[z, u] = sb("w1s%d%d" % (z, u), [P, 2 * P], U8)
             nc.vector.quantize_mx(out=w1c[z, u][:].bitcast(FP8X4), scales=w1s[z, u][:],
                                   in_=staged[z, u][:].rearrange("p t m j -> p (t m j)"))
 
+        def pick(z, a, b):
+            picked = gather("xw%d_%d" % (z, a), U32, xw_all[z][:].bitcast(U32), a, b)
+            for c in range(a, b, P):
+                xw[z, c] = picked[:, c - a : c - a + P]
+            return picked
+
         cast(0, 0, nc.scalar.copy)
-        cast(1, 0, nc.scalar.copy)
-        cast(0, 1, nc.vector.tensor_copy)
+        cast(0, 1, nc.scalar.copy)
         quant_w1(0, 0)
         quant_w1(0, 1)
+        pick(0, 0, 512)
+        late0 = pick(0, 512, 1024)
+        cast(1, 0, nc.scalar.copy)
         cast(1, 1, nc.vector.tensor_copy)
         quant_w1(1, 1)
         quant_w1(1, 0)
@@ -115,32 +124,28 @@ def tile_picked_route2_mlprelu_p_kernel(tc, x_words, x_scales, gate, w1, w2_word
         nc.sync.dma_start(w2w[:].bitcast(I32), w2_words[0].bitcast(I32))
         nc.sync.dma_start(gate_sb[:], gate)
 
-        xw = {}
 
-        def pick(z, a, b, offset):
-            picked = gather(at(offset, "xw%d_%d" % (z, a), [P, b - a], U32), xw_all[z][:].bitcast(U32), a, b)
-            for c in range(a, b, P):
-                xw[z, c] = picked[:, c - a : c - a + P]
+        warm = bank("warm", 1, [P, 2 * P])
+        for codes, scales in 7 * [(late0[:, : 2 * P], xs[:, 512:768])] + 3 * [(w1c[1, 1][:], w1s[1, 1][:])]:
+            nc.tensor.matmul_mx(out=warm[:], lhsT=w1c[0, 0][:, :P].bitcast(FP8X4), lhsT_scale=w1s[0, 0][:, :P],
+                                rhs=codes.bitcast(FP8X4), rhs_scale=scales, start=True, stop=True)
 
-        pick(0, 0, 512, STAGE[0, 0])
-        pick(1, 0, 256, STAGE[1, 1])
-        pick(1, 256, 512, STAGE[1, 1] + 1024)
-        pick(0, 512, 1024, STAGE[1, 0])
+        pick(1, 0, 256)
+        pick(1, 256, 512)
+        pick(1, 512, 1024)
 
         chunks = ((0, 256), (256, 512), (512, 1024))
-        hb = {0: sb("hb0", [P, P, 4], BF16), 128: at(HB0, "hb128", [P, P, 4], BF16),
-              256: at(STAGE[0, 1], "hb256", [P, 256, 4], BF16), 512: sb("hb512", [P, 512, 4], BF16)}
+        hb = {a: sb("hb%d" % a, [P, b - a, 4], BF16) for a, b in ((0, 128), (128, 256), (256, 512), (512, 1024))}
         hc = {a: sb("hc%d" % a, [P, b - a], U32) for a, b in chunks}
         hs = {a: sb("hs%d" % a, [P, b - a], U8) for a, b in chunks}
 
         def hidden(c, b, a):
             acc = bank("h%d" % c, b, [P, 4, P])
-            half = 512 * (c // 512)
             for t in range(4):
                 cols = slice((t % 2) * P, (t % 2 + 1) * P)
                 for z in range(2):
                     nc.tensor.matmul_mx(out=acc[:, t, :], lhsT=w1c[z, t // 2][:, cols].bitcast(FP8X4), lhsT_scale=w1s[z, t // 2][:, cols],
-                                        rhs=xw[z, c].bitcast(FP8X4), rhs_scale=xs[half][4 * z :, c - half : c - half + P],
+                                        rhs=xw[z, c].bitcast(FP8X4), rhs_scale=xs[4 * z :, c : c + P],
                                         start=(z == 0), stop=(z == 1))
             nc.scalar.activation(out=hb[a][:, c - a : c - a + P, :], in_=acc[:].rearrange("p t n -> p n t"), func=RELU)
 
@@ -148,12 +153,12 @@ def tile_picked_route2_mlprelu_p_kernel(tc, x_words, x_scales, gate, w1, w2_word
             nc.vector.quantize_mx(out=hc[a][:, lo - a : hi - a].bitcast(FP8X4), scales=hs[a][:, lo - a : hi - a],
                                   in_=hb[lo][:].rearrange("p n t -> p (n t)"))
 
-        def result(r, a, e, b, banks=1):
+        def result(r, a, e, b, copy, banks=1):
             acc = bank("y%d_%d" % (r, a), b, [P, 512 * banks])[:, : e - a]
             nc.tensor.matmul_mx(out=acc, lhsT=w2w[:, 2 * P * r : 2 * P * (r + 1)].bitcast(FP4X4), lhsT_scale=w2s[:, P * r : P * (r + 1)],
                                 rhs=hc[a][:].bitcast(FP8X4), rhs_scale=hs[a][:], start=True, stop=True)
             y = sb("y%d_%d" % (r, a), [P, e - a], F32)
-            nc.scalar.copy(y[:], acc)
+            copy(y[:], acc)
             return y
 
         def put(r, a, e, y):
@@ -161,24 +166,20 @@ def tile_picked_route2_mlprelu_p_kernel(tc, x_words, x_scales, gate, w1, w2_word
 
         hidden(0, 0, 0)
         quant(0, 0, 128)
-        hidden(128, 3, 128)
+        hidden(128, 5, 128)
         quant(0, 128, 256)
-        pick(1, 512, 768, HB0)
-        hidden(256, 4, 256)
-        y00 = result(0, 0, 256, 0, banks=3)
+        y00 = result(0, 0, 256, 0, nc.vector.tensor_copy, banks=5)
         put(0, 0, 256, y00)
-        hidden(384, 0, 256)
+        hidden(256, 6, 256)
+        hidden(384, 7, 256)
         quant(256, 256, 512)
-        pick(1, 768, 1024, STAGE[0, 1])
-        put(1, 0, 256, result(1, 0, 256, 0))
-        put(0, 256, 512, result(0, 256, 512, 3))
-        hidden(512, 1, 512)
-        hidden(640, 2, 512)
-        hidden(768, 5, 512)
-        hidden(896, 6, 512)
+        put(1, 0, 256, result(1, 0, 256, 7, nc.scalar.copy))
+        put(0, 256, 512, result(0, 256, 512, 5, nc.scalar.copy))
+        for i in range(4):
+            hidden(512 + P * i, 1 + i, 512)
         quant(512, 512, 1024)
-        put(1, 256, 512, result(1, 256, 512, 6))
-        put(0, 512, 1024, result(0, 512, 1024, 4))
+        put(1, 256, 512, result(1, 256, 512, 4, nc.scalar.copy))
+        put(0, 512, 1024, result(0, 512, 1024, 6, nc.scalar.copy))
         nc.sync.dma_start(out[0:P, :], win[0][:])
-        put(1, 512, 1024, result(1, 512, 1024, 7))
+        put(1, 512, 1024, result(1, 512, 1024, 0, nc.scalar.copy))
         nc.sync.dma_start(out[P : 2 * P, :], win[1][:])

@@ -13,11 +13,27 @@ FP4X4 = mybir.dt.float4_e2m1fn_x4
 RELU = mybir.ActivationFunctionType.Relu
 COPY = mybir.ActivationFunctionType.Copy
 MULT = mybir.AluOpType.mult
+ADD = mybir.AluOpType.add
 
 K, T, S, H, N, U = 1024, 2048, 1024, 512, 256, 2048
 P = 128
+PACK = 4
+K_PASS = P * PACK
+BANK_BYTES = 2048
 FLOPS = 2 * K * H * S + 2 * H * N * S
-LEAD = 96
+
+BIG = 8192
+W1_AT = (0, 2 * BIG)
+W2_SCALES_AT = 3 * BIG
+X_AT = (BIG, W2_SCALES_AT + N)
+ZEROS = 32
+HALF_ZEROS_BYTES = 2 * ZEROS
+
+CHUNKS = ((0, 128), (128, 384), (384, 640), (640, 1024))
+RUNS = ((0, 128), (128, 256), (256, 384), (384, 640), (640, 768), (768, 1024))
+HIDDEN_BANK = (0, 6, 7, 1, 2, 3, 4, 5)
+FIRST_BANKS = 6
+WARM_AFTER_GATHER, WARM_AFTER_QUANTISE = 7, 3
 
 
 def tile_picked_route2_mlprelu_p_kernel(tc, x_words, x_scales, gate, w1, w2_words, w2_scales, offs, dst, out):
@@ -28,158 +44,201 @@ def tile_picked_route2_mlprelu_p_kernel(tc, x_words, x_scales, gate, w1, w2_word
         shared = ctx.enter_context(tc.tile_pool(name="shared", bufs=1))
         psum = ctx.enter_context(tc.psum_pool(name="psum", bufs=1))
 
-        def sb(name, shape, dtype):
+        def own(name, shape, dtype):
             return keep.tile(shape, dtype, name=name, align_bytes=64)
 
         def at(offset, name, shape, dtype):
             return shared.tile(shape, dtype, name=name, offset=offset, align_bytes=64)
 
-        def bank(name, b, shape):
-            return psum.tile(shape, F32, name=name, offset=2048 * b)
+        def bank(name, index, shape):
+            return psum.tile(shape, F32, name=name, offset=BANK_BYTES * index)
 
-        RAW = (0, 16384)
-        XW = (8192, 24576 + N)
-        W2S = 24576
+        def entries(list_tile, a, b):
+            return list_tile[:, a // 16 : b // 16]
+
+        w1_raw, x_all = {}, {}
+
+        def load_w1(z):
+            w1_raw[z] = at(W1_AT[z], "w1_raw%d" % z, [P, PACK, H], F32)
+            nc.sync.dma_start(w1_raw[z][:], w1[K_PASS * z : K_PASS * (z + 1), :].rearrange("(p j) c -> p j c", j=PACK))
+
+        def load_x(z):
+            x_all[z] = at(X_AT[z], "x_all%d" % z, [P, T], I32)
+            nc.sync.dma_start(x_all[z][:], x_words[z].rearrange("p c r -> p (c r)").bitcast(I32))
 
         offs_sb = lists.tile([P, S // 16], U16, name="offs_sb")
         dst_sb = lists.tile([P, S // 16], U16, name="dst_sb")
         nc.sync.dma_start(offs_sb[:], offs)
-        w1_raw, xw_all = {}, {}
-
-        def load_w1(z):
-            w1_raw[z] = at(RAW[z], "w1_raw%d" % z, [P, 4, H], F32)
-            nc.sync.dma_start(w1_raw[z][:], w1[512 * z : 512 * (z + 1), :].rearrange("(p j) c -> p j c", j=4))
-
-        def load_x(z):
-            xw_all[z] = at(XW[z], "xw_all%d" % z, [P, T], I32)
-            nc.sync.dma_start(xw_all[z][:], x_words[z].rearrange("p c r -> p (c r)").bitcast(I32))
-
         load_w1(0)
         nc.sync.dma_start(dst_sb[:], dst)
 
-        xs_all = sb("xs_all", [P, T], U8)
-        nc.vector.memset(xs_all[:].bitcast(I32), 0)
+        x_scales_all = own("x_scales_all", [P, T], U8)
+        nc.vector.memset(x_scales_all[:].bitcast(I32), 0)
         for q in range(4):
-            nc.scalar.dma_start(xs_all[32 * q : 32 * q + 8, :].bitcast(I32), x_scales[:, 4 * q : 4 * q + 4, :].bitcast(I32))
+            nc.scalar.dma_start(
+                x_scales_all[32 * q : 32 * q + 8, :].bitcast(I32), x_scales[:, 4 * q : 4 * q + 4, :].bitcast(I32)
+            )
 
-        win = [sb("win%d" % b, [P, U], F32) for b in range(2)]
-        zero_v = at(RAW[1] - 64, "zero_v", [P, 32], F32)
-        zero_s = at(W2S + N - 64, "zero_s", [P, 32], F32)
-        nc.vector.memset(zero_v[:], 0.0)
-        nc.vector.memset(zero_s[:], 0.0)
-        nc.scalar.activation(out=win[1][:, :32], in_=zero_s[:], func=COPY)
-        nc.vector.tensor_copy(win[0][:].rearrange("p (a b) -> p a b", b=32), zero_v[:].unsqueeze(1).to_broadcast([P, U // 32, 32]))
-        nc.vector.tensor_copy(win[1][:, 32:], win[0][:, 32:])
+        window = [own("window%d" % r, [P, U], F32) for r in range(2)]
+        zeros_v = at(W1_AT[1] - HALF_ZEROS_BYTES, "zeros_v", [P, ZEROS], F32)
+        zeros_s = at(X_AT[1] - HALF_ZEROS_BYTES, "zeros_s", [P, ZEROS], F32)
+        nc.vector.memset(zeros_v[:], 0.0)
+        nc.vector.memset(zeros_s[:], 0.0)
+        nc.scalar.activation(out=window[1][:, :ZEROS], in_=zeros_s[:], func=COPY)
+        nc.vector.tensor_copy(
+            window[0][:].rearrange("p (a b) -> p a b", b=ZEROS),
+            zeros_v[:].unsqueeze(1).to_broadcast([P, U // ZEROS, ZEROS]),
+        )
+        nc.vector.tensor_copy(window[1][:, ZEROS:], window[0][:, ZEROS:])
+
+        zero_addend = own("zero_addend", [P, P], F32)
+        nc.gpsimd.memset(zero_addend[:], 0.0)
 
         load_x(0)
         load_w1(1)
         load_x(1)
-        w2s = at(W2S, "w2s", [P, N], U8)
-        nc.gpsimd.memset(w2s[:].bitcast(I32), 0)
+        w2_scales_sb = at(W2_SCALES_AT, "w2_scales_sb", [P, N], U8)
+        nc.gpsimd.memset(w2_scales_sb[:].bitcast(I32), 0)
         for q in range(4):
-            nc.sync.dma_start(w2s[32 * q : 32 * q + 4, :].bitcast(I32), w2_scales[0, 4 * q : 4 * q + 4, :].bitcast(I32))
+            nc.sync.dma_start(
+                w2_scales_sb[32 * q : 32 * q + 4, :].bitcast(I32), w2_scales[0, 4 * q : 4 * q + 4, :].bitcast(I32)
+            )
 
-        def entries(lst, a, b):
-            return lst[:, a // 16 : b // 16]
-
-        def gather(name, dtype, window, a, b):
-            picked = sb(name, [P, b - a], dtype)
-            nc.vector.tensor_copy(picked[:], window.indirect(entries(offs_sb, a, b)))
+        def gather(name, dtype, source, a, b):
+            picked = own(name, [P, b - a], dtype)
+            nc.vector.tensor_copy(picked[:], source.indirect(entries(offs_sb, a, b)))
             return picked
 
-        xs = gather("xs", U8, xs_all[:], 0, S)
+        x_scale = gather("x_scale", U8, x_scales_all[:], 0, S)
 
-        w1c, w1s, staged, xw = {}, {}, {}, {}
+        w1_bf16, w1_code, w1_scale, x_word = {}, {}, {}, {}
 
-        def cast(z, u, copy):
-            staged[z, u] = sb("w1_bf%d%d" % (z, u), [P, 2, P, 4], BF16)
-            copy(staged[z, u][:].rearrange("p t m j -> p m t j"),
-                 w1_raw[z][:].rearrange("p j (m t) -> p m t j", t=4)[:, :, 2 * u : 2 * u + 2, :])
+        def round_w1(z, u, copy):
+            w1_bf16[z, u] = own("w1_bf16_%d%d" % (z, u), [P, 2, P, PACK], BF16)
+            copy(
+                w1_bf16[z, u][:].rearrange("p t m j -> p m t j"),
+                w1_raw[z][:].rearrange("p j (m t) -> p m t j", t=PACK)[:, :, 2 * u : 2 * u + 2, :],
+            )
 
-        def quant_w1(z, u):
-            w1c[z, u] = sb("w1c%d%d" % (z, u), [P, 2 * P], U32)
-            w1s[z, u] = sb("w1s%d%d" % (z, u), [P, 2 * P], U8)
-            nc.vector.quantize_mx(out=w1c[z, u][:].bitcast(FP8X4), scales=w1s[z, u][:],
-                                  in_=staged[z, u][:].rearrange("p t m j -> p (t m j)"))
+        def quantise_w1(z, u):
+            w1_code[z, u] = own("w1_code%d%d" % (z, u), [P, 2 * P], U32)
+            w1_scale[z, u] = own("w1_scale%d%d" % (z, u), [P, 2 * P], U8)
+            nc.vector.quantize_mx(
+                out=w1_code[z, u][:].bitcast(FP8X4),
+                scales=w1_scale[z, u][:],
+                in_=w1_bf16[z, u][:].rearrange("p t m j -> p (t m j)"),
+            )
 
-        def pick(z, a, b):
-            picked = gather("xw%d_%d" % (z, a), U32, xw_all[z][:].bitcast(U32), a, b)
+        def gather_words(z, a, b):
+            picked = gather("x_word%d_%d" % (z, a), U32, x_all[z][:].bitcast(U32), a, b)
             for c in range(a, b, P):
-                xw[z, c] = picked[:, c - a : c - a + P]
+                x_word[z, c] = picked[:, c - a : c - a + P]
             return picked
 
-        cast(0, 0, nc.scalar.copy)
-        cast(0, 1, nc.scalar.copy)
-        quant_w1(0, 0)
-        quant_w1(0, 1)
-        pick(0, 0, 512)
-        late0 = pick(0, 512, 1024)
-        cast(1, 0, nc.scalar.copy)
-        cast(1, 1, nc.vector.tensor_copy)
-        quant_w1(1, 1)
-        quant_w1(1, 0)
+        round_w1(0, 0, nc.scalar.copy)
+        round_w1(0, 1, nc.scalar.copy)
+        quantise_w1(0, 0)
+        quantise_w1(0, 1)
+        gather_words(0, 0, S // 2)
+        upper_words = gather_words(0, S // 2, S)
+        round_w1(1, 0, nc.scalar.copy)
+        round_w1(1, 1, nc.vector.tensor_copy)
+        quantise_w1(1, 1)
+        quantise_w1(1, 0)
 
-        gate_sb = at(RAW[0], "gate_sb", [P, S], F32)
-        w2w = at(RAW[0] + 4 * S, "w2w", [P, 2 * N], U8)
-        nc.sync.dma_start(w2w[:].bitcast(I32), w2_words[0].bitcast(I32))
+        gate_sb = at(W1_AT[0], "gate_sb", [P, S], F32)
+        w2_words_sb = at(W1_AT[0] + 4 * S, "w2_words_sb", [P, 2 * N], U8)
+        nc.sync.dma_start(w2_words_sb[:].bitcast(I32), w2_words[0].bitcast(I32))
         nc.sync.dma_start(gate_sb[:], gate)
 
-
         warm = bank("warm", 1, [P, 2 * P])
-        for codes, scales in 7 * [(late0[:, : 2 * P], xs[:, 512:768])] + 3 * [(w1c[1, 1][:], w1s[1, 1][:])]:
-            nc.tensor.matmul_mx(out=warm[:], lhsT=w1c[0, 0][:, :P].bitcast(FP8X4), lhsT_scale=w1s[0, 0][:, :P],
-                                rhs=codes.bitcast(FP8X4), rhs_scale=scales, start=True, stop=True)
+        after_gather = (upper_words[:, : 2 * P], x_scale[:, S // 2 : S // 2 + 2 * P])
+        after_quantise = (w1_code[1, 1][:], w1_scale[1, 1][:])
+        for codes, scales in WARM_AFTER_GATHER * [after_gather] + WARM_AFTER_QUANTISE * [after_quantise]:
+            nc.tensor.matmul_mx(
+                out=warm[:],
+                lhsT=w1_code[0, 0][:, :P].bitcast(FP8X4),
+                lhsT_scale=w1_scale[0, 0][:, :P],
+                rhs=codes.bitcast(FP8X4),
+                rhs_scale=scales,
+                start=True,
+                stop=True,
+            )
 
-        pick(1, 0, 256)
-        pick(1, 256, 512)
-        pick(1, 512, 1024)
+        gather_words(1, 0, S // 4)
+        gather_words(1, S // 4, S // 2)
+        gather_words(1, S // 2, S)
 
-        chunks = ((0, 256), (256, 512), (512, 1024))
-        hb = {a: sb("hb%d" % a, [P, b - a, 4], BF16) for a, b in ((0, 128), (128, 256), (256, 512), (512, 1024))}
-        hc = {a: sb("hc%d" % a, [P, b - a], U32) for a, b in chunks}
-        hs = {a: sb("hs%d" % a, [P, b - a], U8) for a, b in chunks}
+        h_bf16 = {a: own("h_bf16_%d" % a, [P, b - a, PACK], BF16) for a, b in RUNS}
+        h_code = {a: own("h_code%d" % a, [P, b - a], U32) for a, b in CHUNKS}
+        h_scale = {a: own("h_scale%d" % a, [P, b - a], U8) for a, b in CHUNKS}
 
-        def hidden(c, b, a):
-            acc = bank("h%d" % c, b, [P, 4, P])
-            for t in range(4):
-                cols = slice((t % 2) * P, (t % 2 + 1) * P)
-                for z in range(2):
-                    nc.tensor.matmul_mx(out=acc[:, t, :], lhsT=w1c[z, t // 2][:, cols].bitcast(FP8X4), lhsT_scale=w1s[z, t // 2][:, cols],
-                                        rhs=xw[z, c].bitcast(FP8X4), rhs_scale=xs[4 * z :, c : c + P],
-                                        start=(z == 0), stop=(z == 1))
-            nc.scalar.activation(out=hb[a][:, c - a : c - a + P, :], in_=acc[:].rearrange("p t n -> p n t"), func=RELU)
+        def hidden_run(chunk, run):
+            a, (lo, hi) = chunk[0], run
+            for c in range(lo, hi, P):
+                acc = bank("h%d" % c, HIDDEN_BANK[c // P], [P, PACK, P])
+                for t in range(PACK):
+                    cols = slice((t % 2) * P, (t % 2 + 1) * P)
+                    for z in range(2):
+                        nc.tensor.matmul_mx(
+                            out=acc[:, t, :],
+                            lhsT=w1_code[z, t // 2][:, cols].bitcast(FP8X4),
+                            lhsT_scale=w1_scale[z, t // 2][:, cols],
+                            rhs=x_word[z, c].bitcast(FP8X4),
+                            rhs_scale=x_scale[4 * z :, c : c + P],
+                            start=(z == 0),
+                            stop=(z == 1),
+                        )
+                nc.scalar.activation(
+                    out=h_bf16[lo][:, c - lo : c - lo + P, :], in_=acc[:].rearrange("p t n -> p n t"), func=RELU
+                )
+            nc.vector.quantize_mx(
+                out=h_code[a][:, lo - a : hi - a].bitcast(FP8X4),
+                scales=h_scale[a][:, lo - a : hi - a],
+                in_=h_bf16[lo][:].rearrange("p n t -> p (n t)"),
+            )
 
-        def quant(a, lo, hi):
-            nc.vector.quantize_mx(out=hc[a][:, lo - a : hi - a].bitcast(FP8X4), scales=hs[a][:, lo - a : hi - a],
-                                  in_=hb[lo][:].rearrange("p n t -> p (n t)"))
+        def second_layer(acc, r, a, lo, hi):
+            nc.tensor.matmul_mx(
+                out=acc,
+                lhsT=w2_words_sb[:, 2 * P * r : 2 * P * (r + 1)].bitcast(FP4X4),
+                lhsT_scale=w2_scales_sb[:, P * r : P * (r + 1)],
+                rhs=h_code[a][:, lo - a : hi - a].bitcast(FP8X4),
+                rhs_scale=h_scale[a][:, lo - a : hi - a],
+                start=True,
+                stop=True,
+            )
 
-        def result(r, a, e, b, copy, banks=1):
-            acc = bank("y%d_%d" % (r, a), b, [P, 512 * banks])[:, : e - a]
-            nc.tensor.matmul_mx(out=acc, lhsT=w2w[:, 2 * P * r : 2 * P * (r + 1)].bitcast(FP4X4), lhsT_scale=w2s[:, P * r : P * (r + 1)],
-                                rhs=hc[a][:].bitcast(FP8X4), rhs_scale=hs[a][:], start=True, stop=True)
-            y = sb("y%d_%d" % (r, a), [P, e - a], F32)
-            copy(y[:], acc)
-            return y
+        def finish(r, chunk, bank_index):
+            a, b = chunk
+            acc = bank("y%d_%d" % (r, a), bank_index, [P, b - a])
+            for lo in range(a, b, 2 * P):
+                hi = min(lo + 2 * P, b)
+                second_layer(acc[:, lo - a : hi - a], r, a, lo, hi)
+            y = own("y%d_%d" % (r, a), [P, b - a], F32)
+            nc.scalar.copy(y[:], acc[:])
+            nc.vector.tensor_tensor(window[r][:].indirect(entries(dst_sb, a, b)), y[:], gate_sb[:, a:b], MULT)
 
-        def put(r, a, e, y):
-            nc.vector.tensor_tensor(win[r][:].indirect(entries(dst_sb, a, e)), y[:], gate_sb[:, a:e], MULT)
+        hidden_run(CHUNKS[0], RUNS[0])
+        first = bank("first", 0, [P, FIRST_BANKS * PACK, P])
+        gated = own("gated", [P, 2, P], F32)
+        for r in range(2):
+            second_layer(first[:, r, :], r, 0, 0, P)
+        for r in range(2):
+            nc.vector.tensor_tensor(gated[:, r, :], first[:, r, :], gate_sb[:, :P], MULT)
+        hidden_run(CHUNKS[1], RUNS[1])
+        hidden_run(CHUNKS[1], RUNS[2])
+        for r in range(2):
+            nc.vector.tensor_tensor(window[r][:].indirect(entries(dst_sb, 0, P)), gated[:, r, :], zero_addend[:], ADD)
 
-        hidden(0, 0, 0)
-        quant(0, 0, 128)
-        hidden(128, 5, 128)
-        quant(0, 128, 256)
-        y00 = result(0, 0, 256, 0, nc.vector.tensor_copy, banks=5)
-        put(0, 0, 256, y00)
-        hidden(256, 6, 256)
-        hidden(384, 7, 256)
-        quant(256, 256, 512)
-        put(1, 0, 256, result(1, 0, 256, 7, nc.scalar.copy))
-        put(0, 256, 512, result(0, 256, 512, 5, nc.scalar.copy))
-        for i in range(4):
-            hidden(512 + P * i, 1 + i, 512)
-        quant(512, 512, 1024)
-        put(1, 256, 512, result(1, 256, 512, 4, nc.scalar.copy))
-        put(0, 512, 1024, result(0, 512, 1024, 6, nc.scalar.copy))
-        nc.sync.dma_start(out[0:P, :], win[0][:])
-        put(1, 512, 1024, result(1, 512, 1024, 0, nc.scalar.copy))
-        nc.sync.dma_start(out[P : 2 * P, :], win[1][:])
+        finish(0, CHUNKS[1], HIDDEN_BANK[1])
+        hidden_run(CHUNKS[2], RUNS[3])
+        finish(1, CHUNKS[1], HIDDEN_BANK[4])
+        finish(0, CHUNKS[2], HIDDEN_BANK[2])
+        hidden_run(CHUNKS[3], RUNS[4])
+        hidden_run(CHUNKS[3], RUNS[5])
+        finish(1, CHUNKS[2], HIDDEN_BANK[7])
+        finish(0, CHUNKS[3], HIDDEN_BANK[0])
+        nc.sync.dma_start(out[:P, :], window[0][:])
+        finish(1, CHUNKS[3], HIDDEN_BANK[3])
+        nc.sync.dma_start(out[P:, :], window[1][:])

@@ -26,6 +26,7 @@ BIG = 8192
 W1_AT = (0, 2 * BIG)
 W2_SCALES_AT = 3 * BIG
 X_AT = (BIG, W2_SCALES_AT + N)
+ZEROS_FIRST_AT = BIG - 64
 ZEROS = 32
 HALF_ZEROS_BYTES = 2 * ZEROS
 
@@ -58,9 +59,10 @@ def tile_picked_route2_mlprelu_p_kernel(tc, x_words, x_scales, gate, w1, w2_word
 
         w1_raw, x_all = {}, {}
 
-        def load_w1(z):
-            w1_raw[z] = at(W1_AT[z], "w1_raw%d" % z, [P, PACK, H], F32)
-            nc.sync.dma_start(w1_raw[z][:], w1[K_PASS * z : K_PASS * (z + 1), :].rearrange("(p j) c -> p j c", j=PACK))
+        def load_w1(z, first, last):
+            w1_raw[z, first] = at(W1_AT[z] + 4 * H * first, "w1_raw%d%d" % (z, first), [P, last - first, H], F32)
+            rows = w1[K_PASS * z : K_PASS * (z + 1), :].rearrange("(p j) c -> p j c", j=PACK)
+            nc.sync.dma_start(w1_raw[z, first][:], rows[:, first:last, :])
 
         def load_x(z):
             x_all[z] = at(X_AT[z], "x_all%d" % z, [P, T], I32)
@@ -69,33 +71,40 @@ def tile_picked_route2_mlprelu_p_kernel(tc, x_words, x_scales, gate, w1, w2_word
         offs_sb = lists.tile([P, S // 16], U16, name="offs_sb")
         dst_sb = lists.tile([P, S // 16], U16, name="dst_sb")
         nc.sync.dma_start(offs_sb[:], offs)
-        load_w1(0)
+        load_w1(0, 0, 2)
         nc.sync.dma_start(dst_sb[:], dst)
 
         x_scales_all = own("x_scales_all", [P, T], U8)
         nc.vector.memset(x_scales_all[:].bitcast(I32), 0)
         for q in range(4):
-            nc.scalar.dma_start(
+            nc.sync.dma_start(
                 x_scales_all[32 * q : 32 * q + 8, :].bitcast(I32), x_scales[:, 4 * q : 4 * q + 4, :].bitcast(I32)
             )
 
         window = [own("window%d" % r, [P, U], F32) for r in range(2)]
         zeros_v = at(W1_AT[1] - HALF_ZEROS_BYTES, "zeros_v", [P, ZEROS], F32)
         zeros_s = at(X_AT[1] - HALF_ZEROS_BYTES, "zeros_s", [P, ZEROS], F32)
+        zeros_first = at(ZEROS_FIRST_AT, "zeros_first", [P, ZEROS], F32)
+        nc.vector.memset(zeros_first[:], 0.0)
+        nc.vector.tensor_copy(
+            window[0][:, : 2 * ZEROS].rearrange("p (a b) -> p a b", b=ZEROS),
+            zeros_first[:].unsqueeze(1).to_broadcast([P, 2, ZEROS]),
+        )
         nc.vector.memset(zeros_v[:], 0.0)
         nc.vector.memset(zeros_s[:], 0.0)
         nc.scalar.activation(out=window[1][:, :ZEROS], in_=zeros_s[:], func=COPY)
         nc.vector.tensor_copy(
-            window[0][:].rearrange("p (a b) -> p a b", b=ZEROS),
-            zeros_v[:].unsqueeze(1).to_broadcast([P, U // ZEROS, ZEROS]),
+            window[0][:, 2 * ZEROS :].rearrange("p (a b) -> p a b", b=ZEROS),
+            zeros_v[:].unsqueeze(1).to_broadcast([P, U // ZEROS - 2, ZEROS]),
         )
         nc.vector.tensor_copy(window[1][:, ZEROS:], window[0][:, ZEROS:])
 
         zero_addend = own("zero_addend", [P, P], F32)
         nc.gpsimd.memset(zero_addend[:], 0.0)
 
+        load_w1(0, 2, 4)
         load_x(0)
-        load_w1(1)
+        load_w1(1, 0, 4)
         load_x(1)
         w2_scales_sb = at(W2_SCALES_AT, "w2_scales_sb", [P, N], U8)
         nc.gpsimd.memset(w2_scales_sb[:].bitcast(I32), 0)
@@ -113,11 +122,12 @@ def tile_picked_route2_mlprelu_p_kernel(tc, x_words, x_scales, gate, w1, w2_word
 
         w1_bf16, w1_code, w1_scale, x_word = {}, {}, {}, {}
 
-        def round_w1(z, u, copy):
-            w1_bf16[z, u] = own("w1_bf16_%d%d" % (z, u), [P, 2, P, PACK], BF16)
+        def round_w1(z, u, copy, first=0, last=PACK):
+            if first == 0:
+                w1_bf16[z, u] = own("w1_bf16_%d%d" % (z, u), [P, 2, P, PACK], BF16)
             copy(
-                w1_bf16[z, u][:].rearrange("p t m j -> p m t j"),
-                w1_raw[z][:].rearrange("p j (m t) -> p m t j", t=PACK)[:, :, 2 * u : 2 * u + 2, :],
+                w1_bf16[z, u][:].rearrange("p t m j -> p m t j")[:, :, :, first:last],
+                w1_raw[z, first][:].rearrange("p j (m t) -> p m t j", t=PACK)[:, :, 2 * u : 2 * u + 2, :],
             )
 
         def quantise_w1(z, u):
@@ -135,11 +145,12 @@ def tile_picked_route2_mlprelu_p_kernel(tc, x_words, x_scales, gate, w1, w2_word
                 x_word[z, c] = picked[:, c - a : c - a + P]
             return picked
 
-        round_w1(0, 0, nc.scalar.copy)
-        round_w1(0, 1, nc.scalar.copy)
+        for first in (0, 2):
+            for u in range(2):
+                round_w1(0, u, nc.scalar.copy, first, first + 2)
         quantise_w1(0, 0)
         quantise_w1(0, 1)
-        gather_words(0, 0, S // 2)
+        lower_words = gather_words(0, 0, S // 2)
         upper_words = gather_words(0, S // 2, S)
         round_w1(1, 0, nc.scalar.copy)
         round_w1(1, 1, nc.vector.tensor_copy)
@@ -151,16 +162,14 @@ def tile_picked_route2_mlprelu_p_kernel(tc, x_words, x_scales, gate, w1, w2_word
         nc.sync.dma_start(w2_words_sb[:].bitcast(I32), w2_words[0].bitcast(I32))
         nc.sync.dma_start(gate_sb[:], gate)
 
-        warm = bank("warm", 1, [P, 2 * P])
-        after_gather = (upper_words[:, : 2 * P], x_scale[:, S // 2 : S // 2 + 2 * P])
-        after_quantise = (w1_code[1, 1][:], w1_scale[1, 1][:])
-        for codes, scales in WARM_AFTER_GATHER * [after_gather] + WARM_AFTER_QUANTISE * [after_quantise]:
+        warm = bank("warm", 1, [P, K_PASS])
+        for quarter, words in [((0, 0), lower_words)] + 2 * [((0, 0), upper_words)] + 2 * [((1, 1), upper_words)]:
             nc.tensor.matmul_mx(
                 out=warm[:],
-                lhsT=w1_code[0, 0][:, :P].bitcast(FP8X4),
-                lhsT_scale=w1_scale[0, 0][:, :P],
-                rhs=codes.bitcast(FP8X4),
-                rhs_scale=scales,
+                lhsT=w1_code[quarter][:, :P].bitcast(FP8X4),
+                lhsT_scale=w1_scale[quarter][:, :P],
+                rhs=words[:].bitcast(FP8X4),
+                rhs_scale=x_scale[:, :K_PASS],
                 start=True,
                 stop=True,
             )

@@ -24,16 +24,17 @@ FLOPS = 2 * K * H * S + 2 * H * N * S
 
 BIG = 8192
 W1_AT = (0, 2 * BIG)
-W2_SCALES_AT = 3 * BIG
-X_AT = (BIG, W2_SCALES_AT + N)
-ZEROS_FIRST_AT = BIG - 64
+X_AT = (BIG, 3 * BIG)
 ZEROS = 32
 HALF_ZEROS_BYTES = 2 * ZEROS
 
 CHUNKS = ((0, 128), (128, 384), (384, 640), (640, 1024))
-RUNS = ((0, 128), (128, 256), (256, 384), (384, 640), (640, 768), (768, 1024))
-HIDDEN_BANK = (0, 6, 7, 1, 2, 3, 4, 5)
-FIRST_BANKS = 6
+RUNS = ((0, 128), (128, 384), (384, 640), (640, 768), (768, 1024))
+HIDDEN_BANK = tuple(range(8))
+HELD_AT = 4 * BIG
+HELD2_AT = 4 * BIG + 1024
+HELD3_AT = 4 * BIG + 4096
+EARLY = 6
 WARM_AFTER_GATHER, WARM_AFTER_QUANTISE = 7, 3
 
 
@@ -82,20 +83,18 @@ def tile_picked_route2_mlprelu_p_kernel(tc, x_words, x_scales, gate, w1, w2_word
             )
 
         window = [own("window%d" % r, [P, U], F32) for r in range(2)]
-        zeros_v = at(W1_AT[1] - HALF_ZEROS_BYTES, "zeros_v", [P, ZEROS], F32)
+        zeros_v = at(X_AT[0] - HALF_ZEROS_BYTES, "zeros_v", [P, ZEROS], F32)
         zeros_s = at(X_AT[1] - HALF_ZEROS_BYTES, "zeros_s", [P, ZEROS], F32)
-        zeros_first = at(ZEROS_FIRST_AT, "zeros_first", [P, ZEROS], F32)
-        nc.vector.memset(zeros_first[:], 0.0)
-        nc.vector.tensor_copy(
-            window[0][:, : 2 * ZEROS].rearrange("p (a b) -> p a b", b=ZEROS),
-            zeros_first[:].unsqueeze(1).to_broadcast([P, 2, ZEROS]),
-        )
         nc.vector.memset(zeros_v[:], 0.0)
         nc.vector.memset(zeros_s[:], 0.0)
+        nc.vector.tensor_copy(
+            window[0][:, : 2 * ZEROS].rearrange("p (a b) -> p a b", b=ZEROS),
+            zeros_v[:].unsqueeze(1).to_broadcast([P, 2, ZEROS]),
+        )
         nc.scalar.activation(out=window[1][:, :ZEROS], in_=zeros_s[:], func=COPY)
         nc.vector.tensor_copy(
             window[0][:, 2 * ZEROS :].rearrange("p (a b) -> p a b", b=ZEROS),
-            zeros_v[:].unsqueeze(1).to_broadcast([P, U // ZEROS - 2, ZEROS]),
+            window[0][:, :ZEROS].unsqueeze(1).to_broadcast([P, U // ZEROS - 2, ZEROS]),
         )
         nc.vector.tensor_copy(window[1][:, ZEROS:], window[0][:, ZEROS:])
 
@@ -106,15 +105,9 @@ def tile_picked_route2_mlprelu_p_kernel(tc, x_words, x_scales, gate, w1, w2_word
         load_x(0)
         load_w1(1, 0, 4)
         load_x(1)
-        w2_scales_sb = at(W2_SCALES_AT, "w2_scales_sb", [P, N], U8)
-        nc.gpsimd.memset(w2_scales_sb[:].bitcast(I32), 0)
-        for q in range(4):
-            nc.sync.dma_start(
-                w2_scales_sb[32 * q : 32 * q + 4, :].bitcast(I32), w2_scales[0, 4 * q : 4 * q + 4, :].bitcast(I32)
-            )
 
-        def gather(name, dtype, source, a, b):
-            picked = own(name, [P, b - a], dtype)
+        def gather(name, dtype, source, a, b, offset=None):
+            picked = own(name, [P, b - a], dtype) if offset is None else at(offset, name, [P, b - a], dtype)
             nc.vector.tensor_copy(picked[:], source.indirect(entries(offs_sb, a, b)))
             return picked
 
@@ -139,8 +132,8 @@ def tile_picked_route2_mlprelu_p_kernel(tc, x_words, x_scales, gate, w1, w2_word
                 in_=w1_bf16[z, u][:].rearrange("p t m j -> p (t m j)"),
             )
 
-        def gather_words(z, a, b):
-            picked = gather("x_word%d_%d" % (z, a), U32, x_all[z][:].bitcast(U32), a, b)
+        def gather_words(z, a, b, offset=None):
+            picked = gather("x_word%d_%d" % (z, a), U32, x_all[z][:].bitcast(U32), a, b, offset)
             for c in range(a, b, P):
                 x_word[z, c] = picked[:, c - a : c - a + P]
             return picked
@@ -150,56 +143,64 @@ def tile_picked_route2_mlprelu_p_kernel(tc, x_words, x_scales, gate, w1, w2_word
                 round_w1(0, u, nc.scalar.copy, first, first + 2)
         quantise_w1(0, 0)
         quantise_w1(0, 1)
-        lower_words = gather_words(0, 0, S // 2)
-        upper_words = gather_words(0, S // 2, S)
+        gather_words(0, 0, S // 2)
+        gather_words(0, S // 2, S)
         round_w1(1, 0, nc.scalar.copy)
         round_w1(1, 1, nc.vector.tensor_copy)
         quantise_w1(1, 1)
         quantise_w1(1, 0)
 
-        gate_sb = at(W1_AT[0], "gate_sb", [P, S], F32)
+        gate_first = at(W1_AT[0], "gate_first", [P, P], F32)
+        gate_sb = at(W1_AT[0] + 4 * P, "gate_sb", [P, S - P], F32)
+        nc.sync.dma_start(gate_first[:], gate[:, :P])
         w2_words_sb = at(W1_AT[0] + 4 * S, "w2_words_sb", [P, 2 * N], U8)
+        w2_scales_sb = at(W1_AT[0] + 4 * S + 2 * N, "w2_scales_sb", [P, N], U8)
+        nc.gpsimd.memset(w2_scales_sb[:].bitcast(I32), 0)
         nc.sync.dma_start(w2_words_sb[:].bitcast(I32), w2_words[0].bitcast(I32))
-        nc.sync.dma_start(gate_sb[:], gate)
-
-        warm = bank("warm", 1, [P, K_PASS])
-        for quarter, words in [((0, 0), lower_words)] + 2 * [((0, 0), upper_words)] + 2 * [((1, 1), upper_words)]:
-            nc.tensor.matmul_mx(
-                out=warm[:],
-                lhsT=w1_code[quarter][:, :P].bitcast(FP8X4),
-                lhsT_scale=w1_scale[quarter][:, :P],
-                rhs=words[:].bitcast(FP8X4),
-                rhs_scale=x_scale[:, :K_PASS],
-                start=True,
-                stop=True,
+        for q in range(4):
+            nc.sync.dma_start(
+                w2_scales_sb[32 * q : 32 * q + 4, :].bitcast(I32), w2_scales[0, 4 * q : 4 * q + 4, :].bitcast(I32)
             )
+        nc.sync.dma_start(gate_sb[:], gate[:, P:])
 
-        gather_words(1, 0, S // 4)
-        gather_words(1, S // 4, S // 2)
-        gather_words(1, S // 2, S)
+        def first_layer(c, z):
+            for t in range(PACK):
+                cols = slice((t % 2) * P, (t % 2 + 1) * P)
+                nc.tensor.matmul_mx(
+                    out=acc[c][:, t, :],
+                    lhsT=w1_code[z, t // 2][:, cols].bitcast(FP8X4),
+                    lhsT_scale=w1_scale[z, t // 2][:, cols],
+                    rhs=x_word[z, c].bitcast(FP8X4),
+                    rhs_scale=x_scale[4 * z :, c : c + P],
+                    start=(z == 0 and t == 0),
+                    stop=(z == 1 and t == PACK - 1),
+                )
 
-        h_bf16 = {a: own("h_bf16_%d" % a, [P, b - a, PACK], BF16) for a, b in RUNS}
-        h_code = {a: own("h_code%d" % a, [P, b - a], U32) for a, b in CHUNKS}
-        h_scale = {a: own("h_scale%d" % a, [P, b - a], U8) for a, b in CHUNKS}
+        acc = {c: bank("h%d" % c, c // P, [P, PACK, P]) for c in range(0, S, P)}
+        for c in range(0, EARLY * P, P):
+            first_layer(c, 0)
+
+        for a in range(0, 3 * S // 4, S // 4):
+            gather_words(1, a, a + S // 4)
+
+        h_bf16 = {a: own("h_bf16_%d" % a, [P, b - a, PACK], BF16) for a, b in RUNS if a not in (0, 384, 640)}
+        h_bf16[640] = at(HELD2_AT + 2048, "h_bf16_640", [P, P, PACK], BF16)
+        h_bf16[384] = at(HELD2_AT, "h_bf16_384", [P, 2 * P, PACK], BF16)
+        h_bf16[0] = at(HELD_AT, "h_bf16_0", [P, P, PACK], BF16)
+        h_code = {a: own("h_code%d" % a, [P, b - a], U32) for a, b in CHUNKS[2:]}
+        h_code[128] = at(HELD3_AT, "h_code128", [P, 2 * P], U32)
+        h_code[0] = at(HELD2_AT + 2048 - 256, "h_code0", [P, P], U32)
+        h_scale = {a: own("h_scale%d" % a, [P, b - a], U8) for a, b in CHUNKS[1:]}
+        h_scale[0] = at(HELD3_AT, "h_scale0", [P, P], U8)
 
         def hidden_run(chunk, run):
             a, (lo, hi) = chunk[0], run
             for c in range(lo, hi, P):
-                acc = bank("h%d" % c, HIDDEN_BANK[c // P], [P, PACK, P])
-                for t in range(PACK):
-                    cols = slice((t % 2) * P, (t % 2 + 1) * P)
-                    for z in range(2):
-                        nc.tensor.matmul_mx(
-                            out=acc[:, t, :],
-                            lhsT=w1_code[z, t // 2][:, cols].bitcast(FP8X4),
-                            lhsT_scale=w1_scale[z, t // 2][:, cols],
-                            rhs=x_word[z, c].bitcast(FP8X4),
-                            rhs_scale=x_scale[4 * z :, c : c + P],
-                            start=(z == 0),
-                            stop=(z == 1),
-                        )
+                if c >= EARLY * P:
+                    first_layer(c, 0)
+                first_layer(c, 1)
                 nc.scalar.activation(
-                    out=h_bf16[lo][:, c - lo : c - lo + P, :], in_=acc[:].rearrange("p t n -> p n t"), func=RELU
+                    out=h_bf16[lo][:, c - lo : c - lo + P, :], in_=acc[c][:].rearrange("p t n -> p n t"), func=RELU
                 )
             nc.vector.quantize_mx(
                 out=h_code[a][:, lo - a : hi - a].bitcast(FP8X4),
@@ -226,26 +227,26 @@ def tile_picked_route2_mlprelu_p_kernel(tc, x_words, x_scales, gate, w1, w2_word
                 second_layer(acc[:, lo - a : hi - a], r, a, lo, hi)
             y = own("y%d_%d" % (r, a), [P, b - a], F32)
             nc.scalar.copy(y[:], acc[:])
-            nc.vector.tensor_tensor(window[r][:].indirect(entries(dst_sb, a, b)), y[:], gate_sb[:, a:b], MULT)
+            nc.vector.tensor_tensor(window[r][:].indirect(entries(dst_sb, a, b)), y[:], gate_sb[:, a - P : b - P], MULT)
 
         hidden_run(CHUNKS[0], RUNS[0])
-        first = bank("first", 0, [P, FIRST_BANKS * PACK, P])
+        gather_words(1, 3 * S // 4, S, HELD_AT)
+        first = [bank("first%d" % r, EARLY + r, [P, P]) for r in range(2)]
         gated = own("gated", [P, 2, P], F32)
         for r in range(2):
-            second_layer(first[:, r, :], r, 0, 0, P)
+            second_layer(first[r][:], r, 0, 0, P)
         for r in range(2):
-            nc.vector.tensor_tensor(gated[:, r, :], first[:, r, :], gate_sb[:, :P], MULT)
+            nc.vector.tensor_tensor(gated[:, r, :], first[r][:], gate_first[:], MULT)
         hidden_run(CHUNKS[1], RUNS[1])
-        hidden_run(CHUNKS[1], RUNS[2])
         for r in range(2):
             nc.vector.tensor_tensor(window[r][:].indirect(entries(dst_sb, 0, P)), gated[:, r, :], zero_addend[:], ADD)
 
         finish(0, CHUNKS[1], HIDDEN_BANK[1])
-        hidden_run(CHUNKS[2], RUNS[3])
+        hidden_run(CHUNKS[2], RUNS[2])
         finish(1, CHUNKS[1], HIDDEN_BANK[4])
         finish(0, CHUNKS[2], HIDDEN_BANK[2])
+        hidden_run(CHUNKS[3], RUNS[3])
         hidden_run(CHUNKS[3], RUNS[4])
-        hidden_run(CHUNKS[3], RUNS[5])
         finish(1, CHUNKS[2], HIDDEN_BANK[7])
         finish(0, CHUNKS[3], HIDDEN_BANK[0])
         nc.sync.dma_start(out[:P, :], window[0][:])

@@ -144,7 +144,7 @@ def tile_picked_route2_mlprelu_p_kernel(tc, x_words, x_scales, gate, w1, w2_word
         quantise_w1(0, 0)
         quantise_w1(0, 1)
         gather_words(0, 0, S // 2)
-        gather_words(0, S // 2, S)
+        upper_words = gather_words(0, S // 2, S)
         round_w1(1, 0, nc.scalar.copy)
         round_w1(1, 1, nc.vector.tensor_copy)
         quantise_w1(1, 1)
@@ -155,7 +155,7 @@ def tile_picked_route2_mlprelu_p_kernel(tc, x_words, x_scales, gate, w1, w2_word
         nc.sync.dma_start(gate_first[:], gate[:, :P])
         w2_words_sb = at(W1_AT[0] + 4 * S, "w2_words_sb", [P, 2 * N], U8)
         w2_scales_sb = at(W1_AT[0] + 4 * S + 2 * N, "w2_scales_sb", [P, N], U8)
-        nc.gpsimd.memset(w2_scales_sb[:].bitcast(I32), 0)
+        nc.vector.memset(w2_scales_sb[:].bitcast(I32), 0)
         nc.sync.dma_start(w2_words_sb[:].bitcast(I32), w2_words[0].bitcast(I32))
         for q in range(4):
             nc.sync.dma_start(
@@ -179,6 +179,18 @@ def tile_picked_route2_mlprelu_p_kernel(tc, x_words, x_scales, gate, w1, w2_word
         acc = {c: bank("h%d" % c, c // P, [P, PACK, P]) for c in range(0, S, P)}
         for c in range(0, EARLY * P, P):
             first_layer(c, 0)
+
+        warm = bank("warm", EARLY + 1, [P, K_PASS])
+        for quarter in ((1, 1), (1, 1), (1, 0)):
+            nc.tensor.matmul_mx(
+                out=warm[:],
+                lhsT=w1_code[quarter][:, :P].bitcast(FP8X4),
+                lhsT_scale=w1_scale[quarter][:, :P],
+                rhs=upper_words[:].bitcast(FP8X4),
+                rhs_scale=x_scale[:, :K_PASS],
+                start=True,
+                stop=True,
+            )
 
         for a in range(0, 3 * S // 4, S // 4):
             gather_words(1, a, a + S // 4)

@@ -101,8 +101,8 @@ def tile_picked_route2_mlprelu_p_kernel(tc, x_words, x_scales, gate, w1, w2_word
         zero_addend = own("zero_addend", [P, P], F32)
         nc.gpsimd.memset(zero_addend[:], 0.0)
 
-        load_w1(0, 2, 4)
         load_x(0)
+        load_w1(0, 2, 4)
         load_w1(1, 0, 4)
         load_x(1)
 
@@ -141,10 +141,9 @@ def tile_picked_route2_mlprelu_p_kernel(tc, x_words, x_scales, gate, w1, w2_word
         for first in (0, 2):
             for u in range(2):
                 round_w1(0, u, nc.scalar.copy, first, first + 2)
+        gather_words(0, 0, S)
         quantise_w1(0, 0)
         quantise_w1(0, 1)
-        gather_words(0, 0, S // 2)
-        upper_words = gather_words(0, S // 2, S)
         round_w1(1, 0, nc.scalar.copy)
         round_w1(1, 1, nc.vector.tensor_copy)
         quantise_w1(1, 1)
@@ -179,18 +178,6 @@ def tile_picked_route2_mlprelu_p_kernel(tc, x_words, x_scales, gate, w1, w2_word
         acc = {c: bank("h%d" % c, c // P, [P, PACK, P]) for c in range(0, S, P)}
         for c in range(0, EARLY * P, P):
             first_layer(c, 0)
-
-        warm = bank("warm", EARLY + 1, [P, K_PASS])
-        for quarter in ((1, 1), (1, 1), (1, 0)):
-            nc.tensor.matmul_mx(
-                out=warm[:],
-                lhsT=w1_code[quarter][:, :P].bitcast(FP8X4),
-                lhsT_scale=w1_scale[quarter][:, :P],
-                rhs=upper_words[:].bitcast(FP8X4),
-                rhs_scale=x_scale[:, :K_PASS],
-                start=True,
-                stop=True,
-            )
 
         for a in range(0, 3 * S // 4, S // 4):
             gather_words(1, a, a + S // 4)
@@ -231,36 +218,44 @@ def tile_picked_route2_mlprelu_p_kernel(tc, x_words, x_scales, gate, w1, w2_word
                 stop=True,
             )
 
-        def finish(r, chunk, bank_index):
+        def result(r, chunk, bank_index, y):
             a, b = chunk
-            acc = bank("y%d_%d" % (r, a), bank_index, [P, b - a])
+            acc_y = bank("y%d_%d" % (r, a), bank_index, [P, b - a])
             for lo in range(a, b, 2 * P):
                 hi = min(lo + 2 * P, b)
-                second_layer(acc[:, lo - a : hi - a], r, a, lo, hi)
+                second_layer(acc_y[:, lo - a : hi - a], r, a, lo, hi)
+            nc.scalar.copy(y, acc_y[:])
+
+        def scatter(r, a, b, y):
+            nc.vector.tensor_tensor(window[r][:].indirect(entries(dst_sb, a, b)), y, gate_sb[:, a - P : b - P], MULT)
+
+        def finish(r, chunk, bank_index):
+            a, b = chunk
             y = own("y%d_%d" % (r, a), [P, b - a], F32)
-            nc.scalar.copy(y[:], acc[:])
-            nc.vector.tensor_tensor(window[r][:].indirect(entries(dst_sb, a, b)), y[:], gate_sb[:, a - P : b - P], MULT)
+            result(r, chunk, bank_index, y[:])
+            scatter(r, a, b, y[:])
 
         hidden_run(CHUNKS[0], RUNS[0])
         gather_words(1, 3 * S // 4, S, HELD_AT)
-        first = [bank("first%d" % r, EARLY + r, [P, P]) for r in range(2)]
+        first = bank("first", EARLY, [P, (8 - EARLY) * PACK, P])
         gated = own("gated", [P, 2, P], F32)
         for r in range(2):
-            second_layer(first[r][:], r, 0, 0, P)
+            second_layer(first[:, r, :], r, 0, 0, P)
         for r in range(2):
-            nc.vector.tensor_tensor(gated[:, r, :], first[r][:], gate_first[:], MULT)
+            nc.vector.tensor_tensor(gated[:, r, :], first[:, r, :], gate_first[:], MULT)
         hidden_run(CHUNKS[1], RUNS[1])
         for r in range(2):
             nc.vector.tensor_tensor(window[r][:].indirect(entries(dst_sb, 0, P)), gated[:, r, :], zero_addend[:], ADD)
 
         finish(0, CHUNKS[1], HIDDEN_BANK[1])
         hidden_run(CHUNKS[2], RUNS[2])
-        finish(1, CHUNKS[1], HIDDEN_BANK[4])
-        finish(0, CHUNKS[2], HIDDEN_BANK[2])
         hidden_run(CHUNKS[3], RUNS[3])
         hidden_run(CHUNKS[3], RUNS[4])
-        finish(1, CHUNKS[2], HIDDEN_BANK[7])
-        finish(0, CHUNKS[3], HIDDEN_BANK[0])
-        nc.sync.dma_start(out[:P, :], window[0][:])
-        finish(1, CHUNKS[3], HIDDEN_BANK[3])
-        nc.sync.dma_start(out[P:, :], window[1][:])
+        finish(1, CHUNKS[1], HIDDEN_BANK[6])
+        a, mid, b = CHUNKS[2][0], CHUNKS[3][0], S
+        for r in range(2):
+            y_last = own("y_last%d" % r, [P, b - a], F32)
+            result(r, CHUNKS[2], HIDDEN_BANK[2 + 2 * r], y_last[:, : mid - a])
+            result(r, CHUNKS[3], HIDDEN_BANK[3 + 2 * r], y_last[:, mid - a :])
+            scatter(r, a, b, y_last[:])
+            nc.sync.dma_start(out[P * r : P * (r + 1), :], window[r][:])

@@ -258,4 +258,5 @@ def tile_picked_route2_mlprelu_p_kernel(tc, x_words, x_scales, gate, w1, w2_word
             result(r, CHUNKS[2], HIDDEN_BANK[2 + 2 * r], y_last[:, : mid - a])
             result(r, CHUNKS[3], HIDDEN_BANK[3 + 2 * r], y_last[:, mid - a :])
             scatter(r, a, b, y_last[:])
-            nc.sync.dma_start(out[P * r : P * (r + 1), :], window[r][:])
+            nc.sync.dma_start(out[P * r : P * (r + 1), : U // 2], window[r][:, : U // 2])
+            nc.scalar.dma_start(out[P * r : P * (r + 1), U // 2 :], window[r][:, U // 2 :])

@@ -72,14 +72,19 @@ def tile_picked_route2_mlprelu_p_kernel(tc, x_words, x_scales, gate, w1, w2_word
         offs_sb = lists.tile([P, S // 16], U16, name="offs_sb")
         dst_sb = lists.tile([P, S // 16], U16, name="dst_sb")
         nc.sync.dma_start(offs_sb[:], offs)
-        load_w1(0, 0, 2)
         nc.sync.dma_start(dst_sb[:], dst)
+        load_w1(0, 0, 2)
 
         x_scales_all = own("x_scales_all", [P, T], U8)
         nc.vector.memset(x_scales_all[:].bitcast(I32), 0)
-        for q in range(4):
+        for q in range(2):
             nc.sync.dma_start(
                 x_scales_all[32 * q : 32 * q + 8, :].bitcast(I32), x_scales[:, 4 * q : 4 * q + 4, :].bitcast(I32)
+            )
+        for z, q in ((0, 2), (1, 3), (1, 2), (0, 3)):
+            nc.sync.dma_start(
+                x_scales_all[32 * q + 4 * z : 32 * q + 4 * z + 4, :].bitcast(I32),
+                x_scales[z, 4 * q : 4 * q + 4, :].bitcast(I32),
             )
 
         window = [own("window%d" % r, [P, U], F32) for r in range(2)]

@@ -13,7 +13,6 @@ FP4X4 = mybir.dt.float4_e2m1fn_x4
 RELU = mybir.ActivationFunctionType.Relu
 COPY = mybir.ActivationFunctionType.Copy
 MULT = mybir.AluOpType.mult
-ADD = mybir.AluOpType.add
 
 K, T, S, H, N, U = 1024, 2048, 1024, 512, 256, 2048
 P = 128
@@ -28,14 +27,10 @@ X_AT = (BIG, 3 * BIG)
 ZEROS = 32
 HALF_ZEROS_BYTES = 2 * ZEROS
 
-CHUNKS = ((0, 128), (128, 384), (384, 640), (640, 1024))
-RUNS = ((0, 128), (128, 384), (384, 640), (640, 768), (768, 1024))
-HIDDEN_BANK = tuple(range(8))
-HELD_AT = 4 * BIG
-HELD2_AT = 4 * BIG + 1024
-HELD3_AT = 4 * BIG + 4096
-EARLY = 6
-WARM_AFTER_GATHER, WARM_AFTER_QUANTISE = 7, 3
+CHUNK = 256
+GATHERS = (0, 128, 384, 768, 1024)
+SCATTERS = (0, 256, 640, 1024)
+VECTOR_RELU = (3,)
 
 
 def tile_picked_route2_mlprelu_p_kernel(tc, x_words, x_scales, gate, w1, w2_words, w2_scales, offs, dst, out):
@@ -103,9 +98,6 @@ def tile_picked_route2_mlprelu_p_kernel(tc, x_words, x_scales, gate, w1, w2_word
         )
         nc.vector.tensor_copy(window[1][:, ZEROS:], window[0][:, ZEROS:])
 
-        zero_addend = own("zero_addend", [P, P], F32)
-        nc.gpsimd.memset(zero_addend[:], 0.0)
-
         load_x(0)
         load_w1(0, 2, 4)
         load_w1(1, 0, 4)
@@ -154,9 +146,7 @@ def tile_picked_route2_mlprelu_p_kernel(tc, x_words, x_scales, gate, w1, w2_word
         quantise_w1(1, 1)
         quantise_w1(1, 0)
 
-        gate_first = at(W1_AT[0], "gate_first", [P, P], F32)
-        gate_sb = at(W1_AT[0] + 4 * P, "gate_sb", [P, S - P], F32)
-        nc.sync.dma_start(gate_first[:], gate[:, :P])
+        gate_sb = at(W1_AT[0], "gate_sb", [P, S], F32)
         w2_words_sb = at(W1_AT[0] + 4 * S, "w2_words_sb", [P, 2 * N], U8)
         w2_scales_sb = at(W1_AT[0] + 4 * S + 2 * N, "w2_scales_sb", [P, N], U8)
         nc.vector.memset(w2_scales_sb[:].bitcast(I32), 0)
@@ -165,7 +155,7 @@ def tile_picked_route2_mlprelu_p_kernel(tc, x_words, x_scales, gate, w1, w2_word
             nc.sync.dma_start(
                 w2_scales_sb[32 * q : 32 * q + 4, :].bitcast(I32), w2_scales[0, 4 * q : 4 * q + 4, :].bitcast(I32)
             )
-        nc.sync.dma_start(gate_sb[:], gate[:, P:])
+        nc.sync.dma_start(gate_sb[:], gate)
 
         def first_layer(c, z):
             for t in range(PACK):
@@ -181,87 +171,58 @@ def tile_picked_route2_mlprelu_p_kernel(tc, x_words, x_scales, gate, w1, w2_word
                 )
 
         acc = {c: bank("h%d" % c, c // P, [P, PACK, P]) for c in range(0, S, P)}
-        for c in range(0, EARLY * P, P):
+        for c in range(0, S, P):
             first_layer(c, 0)
 
-        for a in range(0, 3 * S // 4, S // 4):
-            gather_words(1, a, a + S // 4)
+        for a, b in zip(GATHERS, GATHERS[1:]):
+            gather_words(1, a, b)
+        for c in range(0, S, P):
+            first_layer(c, 1)
 
-        h_bf16 = {a: own("h_bf16_%d" % a, [P, b - a, PACK], BF16) for a, b in RUNS if a not in (0, 384, 640)}
-        h_bf16[640] = at(HELD2_AT + 2048, "h_bf16_640", [P, P, PACK], BF16)
-        h_bf16[384] = at(HELD2_AT, "h_bf16_384", [P, 2 * P, PACK], BF16)
-        h_bf16[0] = at(HELD_AT, "h_bf16_0", [P, P, PACK], BF16)
-        h_code = {a: own("h_code%d" % a, [P, b - a], U32) for a, b in CHUNKS[2:]}
-        h_code[128] = at(HELD3_AT, "h_code128", [P, 2 * P], U32)
-        h_code[0] = at(HELD2_AT + 2048 - 256, "h_code0", [P, P], U32)
-        h_scale = {a: own("h_scale%d" % a, [P, b - a], U8) for a, b in CHUNKS[1:]}
-        h_scale[0] = at(HELD3_AT, "h_scale0", [P, P], U8)
+        gated = own("gated", [P, 2, S], F32)
+        h_code, h_scale = {}, {}
 
-        def hidden_run(chunk, run):
-            a, (lo, hi) = chunk[0], run
-            for c in range(lo, hi, P):
-                if c >= EARLY * P:
-                    first_layer(c, 0)
-                first_layer(c, 1)
-                nc.scalar.activation(
-                    out=h_bf16[lo][:, c - lo : c - lo + P, :], in_=acc[c][:].rearrange("p t n -> p n t"), func=RELU
-                )
+        def hidden(a):
+            h_bf16 = own("h_bf16_%d" % a, [P, CHUNK, PACK], BF16)
+            for c in range(a, a + CHUNK, P):
+                dest, sums = h_bf16[:, c - a : c - a + P, :], acc[c][:].rearrange("p t n -> p n t")
+                if c // P in VECTOR_RELU:
+                    nc.vector.tensor_scalar_max(dest, sums, 0.0)
+                else:
+                    nc.scalar.activation(out=dest, in_=sums, func=RELU)
+            h_code[a] = own("h_code%d" % a, [P, CHUNK], U32)
+            h_scale[a] = own("h_scale%d" % a, [P, CHUNK], U8)
             nc.vector.quantize_mx(
-                out=h_code[a][:, lo - a : hi - a].bitcast(FP8X4),
-                scales=h_scale[a][:, lo - a : hi - a],
-                in_=h_bf16[lo][:].rearrange("p n t -> p (n t)"),
+                out=h_code[a][:].bitcast(FP8X4), scales=h_scale[a][:], in_=h_bf16[:].rearrange("p n t -> p (n t)")
             )
 
-        def second_layer(acc, r, a, lo, hi):
-            nc.tensor.matmul_mx(
-                out=acc,
-                lhsT=w2_words_sb[:, 2 * P * r : 2 * P * (r + 1)].bitcast(FP4X4),
-                lhsT_scale=w2_scales_sb[:, P * r : P * (r + 1)],
-                rhs=h_code[a][:, lo - a : hi - a].bitcast(FP8X4),
-                rhs_scale=h_scale[a][:, lo - a : hi - a],
-                start=True,
-                stop=True,
+        def result(a):
+            y = bank("y%d" % a, ((a + 2 * CHUNK) // P - 1) % (S // P), [P, 2, CHUNK])
+            for r in range(2):
+                nc.tensor.matmul_mx(
+                    out=y[:, r, :],
+                    lhsT=w2_words_sb[:, 2 * P * r : 2 * P * (r + 1)].bitcast(FP4X4),
+                    lhsT_scale=w2_scales_sb[:, P * r : P * (r + 1)],
+                    rhs=h_code[a][:].bitcast(FP8X4),
+                    rhs_scale=h_scale[a][:],
+                    start=True,
+                    stop=True,
+                )
+            nc.vector.tensor_tensor(
+                gated[:, :, a : a + CHUNK],
+                y[:],
+                gate_sb[:, a : a + CHUNK].unsqueeze(1).to_broadcast([P, 2, CHUNK]),
+                MULT,
             )
 
-        def result(r, chunk, bank_index, y):
-            a, b = chunk
-            acc_y = bank("y%d_%d" % (r, a), bank_index, [P, b - a])
-            for lo in range(a, b, 2 * P):
-                hi = min(lo + 2 * P, b)
-                second_layer(acc_y[:, lo - a : hi - a], r, a, lo, hi)
-            nc.scalar.copy(y, acc_y[:])
+        hidden(0)
+        for a in range(0, S, CHUNK):
+            if a + CHUNK < S:
+                hidden(a + CHUNK)
+            result(a)
 
-        def scatter(r, a, b, y):
-            nc.vector.tensor_tensor(window[r][:].indirect(entries(dst_sb, a, b)), y, gate_sb[:, a - P : b - P], MULT)
-
-        def finish(r, chunk, bank_index):
-            a, b = chunk
-            y = own("y%d_%d" % (r, a), [P, b - a], F32)
-            result(r, chunk, bank_index, y[:])
-            scatter(r, a, b, y[:])
-
-        hidden_run(CHUNKS[0], RUNS[0])
-        gather_words(1, 3 * S // 4, S, HELD_AT)
-        first = bank("first", EARLY, [P, (8 - EARLY) * PACK, P])
-        gated = own("gated", [P, 2, P], F32)
-        for r in range(2):
-            second_layer(first[:, r, :], r, 0, 0, P)
-        for r in range(2):
-            nc.vector.tensor_tensor(gated[:, r, :], first[:, r, :], gate_first[:], MULT)
-        hidden_run(CHUNKS[1], RUNS[1])
-        for r in range(2):
-            nc.vector.tensor_tensor(window[r][:].indirect(entries(dst_sb, 0, P)), gated[:, r, :], zero_addend[:], ADD)
-
-        finish(0, CHUNKS[1], HIDDEN_BANK[1])
-        hidden_run(CHUNKS[2], RUNS[2])
-        hidden_run(CHUNKS[3], RUNS[3])
-        hidden_run(CHUNKS[3], RUNS[4])
-        finish(1, CHUNKS[1], HIDDEN_BANK[6])
-        a, mid, b = CHUNKS[2][0], CHUNKS[3][0], S
-        for r in range(2):
-            y_last = own("y_last%d" % r, [P, b - a], F32)
-            result(r, CHUNKS[2], HIDDEN_BANK[2 + 2 * r], y_last[:, : mid - a])
-            result(r, CHUNKS[3], HIDDEN_BANK[3 + 2 * r], y_last[:, mid - a :])
-            scatter(r, a, b, y_last[:])
-            nc.sync.dma_start(out[P * r : P * (r + 1), : U // 2], window[r][:, : U // 2])
-            nc.scalar.dma_start(out[P * r : P * (r + 1), U // 2 :], window[r][:, U // 2 :])
+        for a, b in zip(SCATTERS, SCATTERS[1:]):
+            nc.scalar.activation(out=window[1][:].indirect(entries(dst_sb, a, b)), in_=gated[:, 1, a:b], func=COPY)
+        nc.scalar.dma_start(out[P:, :], window[1][:])
+        nc.vector.tensor_copy(window[0][:].indirect(dst_sb[:]), gated[:, 0, :])
+        nc.sync.dma_start(out[:P, :], window[0][:])

@@ -23,14 +23,17 @@ FLOPS = 2 * K * H * S + 2 * H * N * S
 
 BIG = 8192
 W1_AT = (0, 2 * BIG)
-X_AT = (BIG, 3 * BIG)
+W2_AT = 3 * BIG
+X_AT = (BIG, W2_AT + 2 * N)
+ZEROS_S = 160
 ZEROS = 32
 HALF_ZEROS_BYTES = 2 * ZEROS
 
 CHUNK = 256
 GATHERS = (0, 128, 384, 768, 1024)
+EARLY_GATHERS = (0, 256, 640, 1024)
 SCATTERS = (0, 256, 640, 1024)
-VECTOR_RELU = (3,)
+VECTOR_RELU = (384, 896)
 
 
 def tile_picked_route2_mlprelu_p_kernel(tc, x_words, x_scales, gate, w1, w2_words, w2_scales, offs, dst, out):
@@ -84,23 +87,31 @@ def tile_picked_route2_mlprelu_p_kernel(tc, x_words, x_scales, gate, w1, w2_word
 
         window = [own("window%d" % r, [P, U], F32) for r in range(2)]
         zeros_v = at(X_AT[0] - HALF_ZEROS_BYTES, "zeros_v", [P, ZEROS], F32)
-        zeros_s = at(X_AT[1] - HALF_ZEROS_BYTES, "zeros_s", [P, ZEROS], F32)
+        zeros_s = at(W2_AT - HALF_ZEROS_BYTES, "zeros_s", [P, ZEROS_S], F32)
         nc.vector.memset(zeros_v[:], 0.0)
         nc.vector.memset(zeros_s[:], 0.0)
+        w2_scales_sb = own("w2_scales_sb", [P, N], U8)
+        nc.vector.memset(w2_scales_sb[:].bitcast(I32), 0)
         nc.vector.tensor_copy(
             window[0][:, : 2 * ZEROS].rearrange("p (a b) -> p a b", b=ZEROS),
             zeros_v[:].unsqueeze(1).to_broadcast([P, 2, ZEROS]),
         )
-        nc.scalar.activation(out=window[1][:, :ZEROS], in_=zeros_s[:], func=COPY)
+        nc.scalar.activation(out=window[1][:, :ZEROS_S], in_=zeros_s[:], func=COPY)
         nc.vector.tensor_copy(
             window[0][:, 2 * ZEROS :].rearrange("p (a b) -> p a b", b=ZEROS),
             window[0][:, :ZEROS].unsqueeze(1).to_broadcast([P, U // ZEROS - 2, ZEROS]),
         )
-        nc.vector.tensor_copy(window[1][:, ZEROS:], window[0][:, ZEROS:])
+        nc.vector.tensor_copy(window[1][:, ZEROS_S:], window[0][:, ZEROS_S:])
 
-        load_x(0)
         load_w1(0, 2, 4)
+        load_x(0)
         load_w1(1, 0, 4)
+        w2_words_sb = at(W2_AT, "w2_words_sb", [P, 2 * N], U8)
+        nc.sync.dma_start(w2_words_sb[:].bitcast(I32), w2_words[0].bitcast(I32))
+        for q in range(4):
+            nc.sync.dma_start(
+                w2_scales_sb[32 * q : 32 * q + 4, :].bitcast(I32), w2_scales[0, 4 * q : 4 * q + 4, :].bitcast(I32)
+            )
         load_x(1)
 
         def gather(name, dtype, source, a, b, offset=None):
@@ -138,24 +149,19 @@ def tile_picked_route2_mlprelu_p_kernel(tc, x_words, x_scales, gate, w1, w2_word
         for first in (0, 2):
             for u in range(2):
                 round_w1(0, u, nc.scalar.copy, first, first + 2)
-        gather_words(0, 0, S)
         quantise_w1(0, 0)
         quantise_w1(0, 1)
+        for a, b in zip(EARLY_GATHERS, EARLY_GATHERS[1:]):
+            gather_words(0, a, b)
         round_w1(1, 0, nc.scalar.copy)
         round_w1(1, 1, nc.vector.tensor_copy)
         quantise_w1(1, 1)
         quantise_w1(1, 0)
 
-        gate_sb = at(W1_AT[0], "gate_sb", [P, S], F32)
-        w2_words_sb = at(W1_AT[0] + 4 * S, "w2_words_sb", [P, 2 * N], U8)
-        w2_scales_sb = at(W1_AT[0] + 4 * S + 2 * N, "w2_scales_sb", [P, N], U8)
-        nc.vector.memset(w2_scales_sb[:].bitcast(I32), 0)
-        nc.sync.dma_start(w2_words_sb[:].bitcast(I32), w2_words[0].bitcast(I32))
-        for q in range(4):
-            nc.sync.dma_start(
-                w2_scales_sb[32 * q : 32 * q + 4, :].bitcast(I32), w2_scales[0, 4 * q : 4 * q + 4, :].bitcast(I32)
-            )
-        nc.sync.dma_start(gate_sb[:], gate)
+        gate_first = at(W1_AT[0], "gate_first", [P, CHUNK], F32)
+        gate_rest = at(W1_AT[0] + 4 * CHUNK, "gate_rest", [P, S - CHUNK], F32)
+        nc.sync.dma_start(gate_first[:], gate[:, :CHUNK])
+        nc.sync.dma_start(gate_rest[:], gate[:, CHUNK:])
 
         def first_layer(c, z):
             for t in range(PACK):
@@ -176,50 +182,62 @@ def tile_picked_route2_mlprelu_p_kernel(tc, x_words, x_scales, gate, w1, w2_word
 
         for a, b in zip(GATHERS, GATHERS[1:]):
             gather_words(1, a, b)
-        for c in range(0, S, P):
+        for c in range(0, S - CHUNK, P):
             first_layer(c, 1)
 
         gated = own("gated", [P, 2, S], F32)
-        h_code, h_scale = {}, {}
+        h_bf16, h_code, h_scale = {}, {}, {}
 
-        def hidden(a):
-            h_bf16 = own("h_bf16_%d" % a, [P, CHUNK, PACK], BF16)
+        def relu(a):
+            h_bf16[a] = own("h_bf16_%d" % a, [P, CHUNK, PACK], BF16)
             for c in range(a, a + CHUNK, P):
-                dest, sums = h_bf16[:, c - a : c - a + P, :], acc[c][:].rearrange("p t n -> p n t")
-                if c // P in VECTOR_RELU:
+                dest, sums = h_bf16[a][:, c - a : c - a + P, :], acc[c][:].rearrange("p t n -> p n t")
+                if c in VECTOR_RELU:
                     nc.vector.tensor_scalar_max(dest, sums, 0.0)
                 else:
                     nc.scalar.activation(out=dest, in_=sums, func=RELU)
+
+        def quantise_h(a):
             h_code[a] = own("h_code%d" % a, [P, CHUNK], U32)
             h_scale[a] = own("h_scale%d" % a, [P, CHUNK], U8)
             nc.vector.quantize_mx(
-                out=h_code[a][:].bitcast(FP8X4), scales=h_scale[a][:], in_=h_bf16[:].rearrange("p n t -> p (n t)")
+                out=h_code[a][:].bitcast(FP8X4), scales=h_scale[a][:], in_=h_bf16[a][:].rearrange("p n t -> p (n t)")
             )
 
-        def result(a):
-            y = bank("y%d" % a, ((a + 2 * CHUNK) // P - 1) % (S // P), [P, 2, CHUNK])
-            for r in range(2):
-                nc.tensor.matmul_mx(
-                    out=y[:, r, :],
-                    lhsT=w2_words_sb[:, 2 * P * r : 2 * P * (r + 1)].bitcast(FP4X4),
-                    lhsT_scale=w2_scales_sb[:, P * r : P * (r + 1)],
-                    rhs=h_code[a][:].bitcast(FP8X4),
-                    rhs_scale=h_scale[a][:],
-                    start=True,
-                    stop=True,
-                )
-            nc.vector.tensor_tensor(
-                gated[:, :, a : a + CHUNK],
-                y[:],
-                gate_sb[:, a : a + CHUNK].unsqueeze(1).to_broadcast([P, 2, CHUNK]),
-                MULT,
+        def second_layer(y, r, a):
+            nc.tensor.matmul_mx(
+                out=y,
+                lhsT=w2_words_sb[:, 2 * P * r : 2 * P * (r + 1)].bitcast(FP4X4),
+                lhsT_scale=w2_scales_sb[:, P * r : P * (r + 1)],
+                rhs=h_code[a][:].bitcast(FP8X4),
+                rhs_scale=h_scale[a][:],
+                start=True,
+                stop=True,
             )
 
-        hidden(0)
-        for a in range(0, S, CHUNK):
-            if a + CHUNK < S:
-                hidden(a + CHUNK)
-            result(a)
+        def result(r, a, bank_index):
+            y = bank("y%d_%d" % (r, a), bank_index, [P, CHUNK])
+            second_layer(y[:], r, a)
+            nc.vector.tensor_tensor(gated[:, r, a : a + CHUNK], y[:], gate_rest[:, a - CHUNK : a] if a else gate_first[:], MULT)
+
+        c0, c1, c2, c3 = range(0, S, CHUNK)
+        for a in (c0, c1):
+            relu(a)
+            quantise_h(a)
+        result(1, c0, 0)
+        for c in range(c3, S, P):
+            first_layer(c, 1)
+        relu(c2)
+        quantise_h(c2)
+        relu(c3)
+        result(1, c1, 1)
+        result(1, c2, 2)
+        quantise_h(c3)
+        result(0, c0, 3)
+        result(0, c1, 4)
+        result(0, c2, 5)
+        result(0, c3, 6)
+        result(1, c3, 7)
 
         for a, b in zip(SCATTERS, SCATTERS[1:]):
             nc.scalar.activation(out=window[1][:].indirect(entries(dst_sb, a, b)), in_=gated[:, 1, a:b], func=COPY)

@@ -31,7 +31,7 @@ HALF_ZEROS_BYTES = 2 * ZEROS
 
 CHUNK = 256
 GATHERS = (0, 128, 384, 768, 1024)
-EARLY_GATHERS = (0, 256, 640, 1024)
+EARLY_GATHERS = (0, 1024)
 SCATTERS = (0, 256, 640, 1024)
 VECTOR_RELU = (384, 896)
 
@@ -103,8 +103,8 @@ def tile_picked_route2_mlprelu_p_kernel(tc, x_words, x_scales, gate, w1, w2_word
         )
         nc.vector.tensor_copy(window[1][:, ZEROS_S:], window[0][:, ZEROS_S:])
 
-        load_w1(0, 2, 4)
         load_x(0)
+        load_w1(0, 2, 4)
         load_w1(1, 0, 4)
         w2_words_sb = at(W2_AT, "w2_words_sb", [P, 2 * N], U8)
         nc.sync.dma_start(w2_words_sb[:].bitcast(I32), w2_words[0].bitcast(I32))
@@ -149,10 +149,10 @@ def tile_picked_route2_mlprelu_p_kernel(tc, x_words, x_scales, gate, w1, w2_word
         for first in (0, 2):
             for u in range(2):
                 round_w1(0, u, nc.scalar.copy, first, first + 2)
-        quantise_w1(0, 0)
-        quantise_w1(0, 1)
         for a, b in zip(EARLY_GATHERS, EARLY_GATHERS[1:]):
             gather_words(0, a, b)
+        quantise_w1(0, 0)
+        quantise_w1(0, 1)
         round_w1(1, 0, nc.scalar.copy)
         round_w1(1, 1, nc.vector.tensor_copy)
         quantise_w1(1, 1)

@@ -23,9 +23,8 @@ FLOPS = 2 * K * H * S + 2 * H * N * S
 
 BIG = 8192
 W1_AT = (0, 2 * BIG)
-W2_AT = 3 * BIG
-X_AT = (BIG, W2_AT + 2 * N)
-ZEROS_S = 160
+X_AT = (BIG, 3 * BIG)
+ZEROS_S = 32
 ZEROS = 32
 HALF_ZEROS_BYTES = 2 * ZEROS
 
@@ -33,6 +32,7 @@ CHUNK = 256
 GATHERS = (0, 128, 384, 768, 1024)
 EARLY_GATHERS = (0, 1024)
 SCATTERS = (0, 256, 640, 1024)
+SCALAR_ROUNDS = 96
 VECTOR_RELU = (384, 896)
 
 
@@ -87,7 +87,7 @@ def tile_picked_route2_mlprelu_p_kernel(tc, x_words, x_scales, gate, w1, w2_word
 
         window = [own("window%d" % r, [P, U], F32) for r in range(2)]
         zeros_v = at(X_AT[0] - HALF_ZEROS_BYTES, "zeros_v", [P, ZEROS], F32)
-        zeros_s = at(W2_AT - HALF_ZEROS_BYTES, "zeros_s", [P, ZEROS_S], F32)
+        zeros_s = at(X_AT[1] - HALF_ZEROS_BYTES, "zeros_s", [P, ZEROS_S], F32)
         nc.vector.memset(zeros_v[:], 0.0)
         nc.vector.memset(zeros_s[:], 0.0)
         w2_scales_sb = own("w2_scales_sb", [P, N], U8)
@@ -106,8 +106,6 @@ def tile_picked_route2_mlprelu_p_kernel(tc, x_words, x_scales, gate, w1, w2_word
         load_x(0)
         load_w1(0, 2, 4)
         load_w1(1, 0, 4)
-        w2_words_sb = at(W2_AT, "w2_words_sb", [P, 2 * N], U8)
-        nc.sync.dma_start(w2_words_sb[:].bitcast(I32), w2_words[0].bitcast(I32))
         for q in range(4):
             nc.sync.dma_start(
                 w2_scales_sb[32 * q : 32 * q + 4, :].bitcast(I32), w2_scales[0, 4 * q : 4 * q + 4, :].bitcast(I32)
@@ -123,12 +121,12 @@ def tile_picked_route2_mlprelu_p_kernel(tc, x_words, x_scales, gate, w1, w2_word
 
         w1_bf16, w1_code, w1_scale, x_word = {}, {}, {}, {}
 
-        def round_w1(z, u, copy, first=0, last=PACK):
-            if first == 0:
+        def round_w1(z, u, copy, first=0, last=PACK, lo=0, hi=P):
+            if (z, u) not in w1_bf16:
                 w1_bf16[z, u] = own("w1_bf16_%d%d" % (z, u), [P, 2, P, PACK], BF16)
             copy(
-                w1_bf16[z, u][:].rearrange("p t m j -> p m t j")[:, :, :, first:last],
-                w1_raw[z, first][:].rearrange("p j (m t) -> p m t j", t=PACK)[:, :, 2 * u : 2 * u + 2, :],
+                w1_bf16[z, u][:].rearrange("p t m j -> p m t j")[:, lo:hi, :, first:last],
+                w1_raw[z, first][:].rearrange("p j (m t) -> p m t j", t=PACK)[:, lo:hi, 2 * u : 2 * u + 2, :],
             )
 
         def quantise_w1(z, u):
@@ -153,17 +151,20 @@ def tile_picked_route2_mlprelu_p_kernel(tc, x_words, x_scales, gate, w1, w2_word
             gather_words(0, a, b)
         quantise_w1(0, 0)
         quantise_w1(0, 1)
-        round_w1(1, 0, nc.scalar.copy)
+        round_w1(1, 0, nc.scalar.copy, hi=SCALAR_ROUNDS)
         round_w1(1, 1, nc.vector.tensor_copy)
+        round_w1(1, 0, nc.vector.tensor_copy, lo=SCALAR_ROUNDS)
         quantise_w1(1, 1)
         quantise_w1(1, 0)
 
         gate_first = at(W1_AT[0], "gate_first", [P, CHUNK], F32)
         gate_rest = at(W1_AT[0] + 4 * CHUNK, "gate_rest", [P, S - CHUNK], F32)
+        w2_words_sb = at(W1_AT[0] + 4 * S, "w2_words_sb", [P, 2 * N], U8)
+        nc.sync.dma_start(w2_words_sb[:].bitcast(I32), w2_words[0].bitcast(I32))
         nc.sync.dma_start(gate_first[:], gate[:, :CHUNK])
         nc.sync.dma_start(gate_rest[:], gate[:, CHUNK:])
 
-        def first_layer(c, z):
+        def first_layer(c, z, opens):
             for t in range(PACK):
                 cols = slice((t % 2) * P, (t % 2 + 1) * P)
                 nc.tensor.matmul_mx(
@@ -172,18 +173,18 @@ def tile_picked_route2_mlprelu_p_kernel(tc, x_words, x_scales, gate, w1, w2_word
                     lhsT_scale=w1_scale[z, t // 2][:, cols],
                     rhs=x_word[z, c].bitcast(FP8X4),
                     rhs_scale=x_scale[4 * z :, c : c + P],
-                    start=(z == 0 and t == 0),
-                    stop=(z == 1 and t == PACK - 1),
+                    start=(opens and t == 0),
+                    stop=(not opens and t == PACK - 1),
                 )
 
         acc = {c: bank("h%d" % c, c // P, [P, PACK, P]) for c in range(0, S, P)}
-        for c in range(0, S, P):
-            first_layer(c, 0)
+        for c in range(0, S - CHUNK, P):
+            first_layer(c, 0, True)
 
         for a, b in zip(GATHERS, GATHERS[1:]):
             gather_words(1, a, b)
         for c in range(0, S - CHUNK, P):
-            first_layer(c, 1)
+            first_layer(c, 1, False)
 
         gated = own("gated", [P, 2, S], F32)
         h_bf16, h_code, h_scale = {}, {}, {}
@@ -226,7 +227,8 @@ def tile_picked_route2_mlprelu_p_kernel(tc, x_words, x_scales, gate, w1, w2_word
             quantise_h(a)
         result(1, c0, 0)
         for c in range(c3, S, P):
-            first_layer(c, 1)
+            first_layer(c, 1, True)
+            first_layer(c, 0, False)
         relu(c2)
         quantise_h(c2)
         relu(c3)

@@ -24,13 +24,11 @@ FLOPS = 2 * K * H * S + 2 * H * N * S
 BIG = 8192
 W1_AT = (0, 2 * BIG)
 X_AT = (BIG, 3 * BIG)
-ZEROS_S = 32
 ZEROS = 32
 HALF_ZEROS_BYTES = 2 * ZEROS
 
 CHUNK = 256
 GATHERS = (0, 128, 384, 768, 1024)
-EARLY_GATHERS = (0, 1024)
 SCATTERS = (0, 256, 640, 1024)
 SCALAR_ROUNDS = 96
 VECTOR_RELU = (384, 896)
@@ -87,7 +85,7 @@ def tile_picked_route2_mlprelu_p_kernel(tc, x_words, x_scales, gate, w1, w2_word
 
         window = [own("window%d" % r, [P, U], F32) for r in range(2)]
         zeros_v = at(X_AT[0] - HALF_ZEROS_BYTES, "zeros_v", [P, ZEROS], F32)
-        zeros_s = at(X_AT[1] - HALF_ZEROS_BYTES, "zeros_s", [P, ZEROS_S], F32)
+        zeros_s = at(X_AT[1] - HALF_ZEROS_BYTES, "zeros_s", [P, ZEROS], F32)
         nc.vector.memset(zeros_v[:], 0.0)
         nc.vector.memset(zeros_s[:], 0.0)
         w2_scales_sb = own("w2_scales_sb", [P, N], U8)
@@ -96,12 +94,12 @@ def tile_picked_route2_mlprelu_p_kernel(tc, x_words, x_scales, gate, w1, w2_word
             window[0][:, : 2 * ZEROS].rearrange("p (a b) -> p a b", b=ZEROS),
             zeros_v[:].unsqueeze(1).to_broadcast([P, 2, ZEROS]),
         )
-        nc.scalar.activation(out=window[1][:, :ZEROS_S], in_=zeros_s[:], func=COPY)
+        nc.scalar.activation(out=window[1][:, :ZEROS], in_=zeros_s[:], func=COPY)
         nc.vector.tensor_copy(
             window[0][:, 2 * ZEROS :].rearrange("p (a b) -> p a b", b=ZEROS),
             window[0][:, :ZEROS].unsqueeze(1).to_broadcast([P, U // ZEROS - 2, ZEROS]),
         )
-        nc.vector.tensor_copy(window[1][:, ZEROS_S:], window[0][:, ZEROS_S:])
+        nc.vector.tensor_copy(window[1][:, ZEROS:], window[0][:, ZEROS:])
 
         load_x(0)
         load_w1(0, 2, 4)
@@ -112,8 +110,8 @@ def tile_picked_route2_mlprelu_p_kernel(tc, x_words, x_scales, gate, w1, w2_word
             )
         load_x(1)
 
-        def gather(name, dtype, source, a, b, offset=None):
-            picked = own(name, [P, b - a], dtype) if offset is None else at(offset, name, [P, b - a], dtype)
+        def gather(name, dtype, source, a, b):
+            picked = own(name, [P, b - a], dtype)
             nc.vector.tensor_copy(picked[:], source.indirect(entries(offs_sb, a, b)))
             return picked
 
@@ -138,17 +136,15 @@ def tile_picked_route2_mlprelu_p_kernel(tc, x_words, x_scales, gate, w1, w2_word
                 in_=w1_bf16[z, u][:].rearrange("p t m j -> p (t m j)"),
             )
 
-        def gather_words(z, a, b, offset=None):
-            picked = gather("x_word%d_%d" % (z, a), U32, x_all[z][:].bitcast(U32), a, b, offset)
+        def gather_words(z, a, b):
+            picked = gather("x_word%d_%d" % (z, a), U32, x_all[z][:].bitcast(U32), a, b)
             for c in range(a, b, P):
                 x_word[z, c] = picked[:, c - a : c - a + P]
-            return picked
 
         for first in (0, 2):
             for u in range(2):
                 round_w1(0, u, nc.scalar.copy, first, first + 2)
-        for a, b in zip(EARLY_GATHERS, EARLY_GATHERS[1:]):
-            gather_words(0, a, b)
+        gather_words(0, 0, S)
         quantise_w1(0, 0)
         quantise_w1(0, 1)
         round_w1(1, 0, nc.scalar.copy, hi=SCALAR_ROUNDS)
@@ -157,12 +153,11 @@ def tile_picked_route2_mlprelu_p_kernel(tc, x_words, x_scales, gate, w1, w2_word
         quantise_w1(1, 1)
         quantise_w1(1, 0)
 
-        gate_first = at(W1_AT[0], "gate_first", [P, CHUNK], F32)
-        gate_rest = at(W1_AT[0] + 4 * CHUNK, "gate_rest", [P, S - CHUNK], F32)
+        gate_sb = at(W1_AT[0], "gate_sb", [P, S], F32)
         w2_words_sb = at(W1_AT[0] + 4 * S, "w2_words_sb", [P, 2 * N], U8)
         nc.sync.dma_start(w2_words_sb[:].bitcast(I32), w2_words[0].bitcast(I32))
-        nc.sync.dma_start(gate_first[:], gate[:, :CHUNK])
-        nc.sync.dma_start(gate_rest[:], gate[:, CHUNK:])
+        nc.sync.dma_start(gate_sb[:, :CHUNK], gate[:, :CHUNK])
+        nc.sync.dma_start(gate_sb[:, CHUNK:], gate[:, CHUNK:])
 
         def first_layer(c, z, opens):
             for t in range(PACK):
@@ -216,33 +211,46 @@ def tile_picked_route2_mlprelu_p_kernel(tc, x_words, x_scales, gate, w1, w2_word
                 stop=True,
             )
 
-        def result(r, a, bank_index):
-            y = bank("y%d_%d" % (r, a), bank_index, [P, CHUNK])
-            second_layer(y[:], r, a)
-            nc.vector.tensor_tensor(gated[:, r, a : a + CHUNK], y[:], gate_rest[:, a - CHUNK : a] if a else gate_first[:], MULT)
+        def gated_result(r, a, b, bank_index):
+            y = bank("y%d_%d" % (r, a), bank_index, [P, b - a])
+            for c in range(a, b, CHUNK):
+                second_layer(y[:, c - a : c - a + CHUNK], r, c)
+            nc.vector.tensor_tensor(gated[:, r, a:b], y[:], gate_sb[:, a:b], MULT)
 
         c0, c1, c2, c3 = range(0, S, CHUNK)
         for a in (c0, c1):
             relu(a)
             quantise_h(a)
-        result(1, c0, 0)
+        gated_result(1, c0, c1, 0)
         for c in range(c3, S, P):
             first_layer(c, 1, True)
             first_layer(c, 0, False)
         relu(c2)
         quantise_h(c2)
         relu(c3)
-        result(1, c1, 1)
-        result(1, c2, 2)
+        gated_result(1, c1, c3, 1)
         quantise_h(c3)
-        result(0, c0, 3)
-        result(0, c1, 4)
-        result(0, c2, 5)
-        result(0, c3, 6)
-        result(1, c3, 7)
+        gated_result(0, c0, c2, 2)
+        gated_result(1, c3, S, 3)
 
-        for a, b in zip(SCATTERS, SCATTERS[1:]):
+        plain = own("plain", [P, S - c2], F32)
+
+        def scatter_rows_1(a, b):
             nc.scalar.activation(out=window[1][:].indirect(entries(dst_sb, a, b)), in_=gated[:, 1, a:b], func=COPY)
+
+        def plain_result(a, bank_index):
+            y = bank("y0_%d" % a, bank_index, [P, CHUNK])
+            second_layer(y[:], 0, a)
+            nc.scalar.copy(plain[:, a - c2 : a - c2 + CHUNK], y[:])
+
+        s0, s1, s2, s3 = SCATTERS
+        scatter_rows_1(s0, s1)
+        plain_result(c2, 4)
+        scatter_rows_1(s1, s2)
+        plain_result(c3, 5)
+        scatter_rows_1(s2, s3)
         nc.scalar.dma_start(out[P:, :], window[1][:])
-        nc.vector.tensor_copy(window[0][:].indirect(dst_sb[:]), gated[:, 0, :])
+
+        nc.vector.tensor_copy(window[0][:].indirect(entries(dst_sb, c0, c2)), gated[:, 0, :c2])
+        nc.vector.tensor_tensor(window[0][:].indirect(entries(dst_sb, c2, S)), plain[:], gate_sb[:, c2:], MULT)
         nc.sync.dma_start(out[:P, :], window[0][:])

@@ -253,4 +253,5 @@ def tile_picked_route2_mlprelu_p_kernel(tc, x_words, x_scales, gate, w1, w2_word
 
         nc.vector.tensor_copy(window[0][:].indirect(entries(dst_sb, c0, c2)), gated[:, 0, :c2])
         nc.vector.tensor_tensor(window[0][:].indirect(entries(dst_sb, c2, S)), plain[:], gate_sb[:, c2:], MULT)
-        nc.sync.dma_start(out[:P, :], window[0][:])
+        nc.sync.dma_start(out[:P, : U // 2], window[0][:, : U // 2])
+        nc.scalar.dma_start(out[:P, U // 2 :], window[0][:, U // 2 :])

@@ -68,7 +68,6 @@ def tile_picked_route2_mlprelu_p_kernel(tc, x_words, x_scales, gate, w1, w2_word
         offs_sb = lists.tile([P, S // 16], U16, name="offs_sb")
         dst_sb = lists.tile([P, S // 16], U16, name="dst_sb")
         nc.sync.dma_start(offs_sb[:], offs)
-        nc.sync.dma_start(dst_sb[:], dst)
         load_w1(0, 0, 2)
 
         x_scales_all = own("x_scales_all", [P, T], U8)
@@ -96,16 +95,20 @@ def tile_picked_route2_mlprelu_p_kernel(tc, x_words, x_scales, gate, w1, w2_word
         )
         nc.scalar.activation(out=window[1][:, :ZEROS], in_=zeros_s[:], func=COPY)
         nc.vector.tensor_copy(
-            window[0][:, 2 * ZEROS :].rearrange("p (a b) -> p a b", b=ZEROS),
-            window[0][:, :ZEROS].unsqueeze(1).to_broadcast([P, U // ZEROS - 2, ZEROS]),
+            window[0][:, 2 * ZEROS :].rearrange("p (a b) -> p a b", b=2 * ZEROS),
+            window[0][:, : 2 * ZEROS].unsqueeze(1).to_broadcast([P, U // (2 * ZEROS) - 1, 2 * ZEROS]),
         )
-        nc.vector.tensor_copy(window[1][:, ZEROS:], window[0][:, ZEROS:])
+        nc.scalar.activation(
+            out=window[1][:, ZEROS:].rearrange("p (a b) -> p a b", b=ZEROS),
+            in_=window[1][:, :ZEROS].unsqueeze(1).to_broadcast([P, U // ZEROS - 1, ZEROS]),
+            func=COPY,
+        )
 
         load_x(0)
         load_w1(0, 2, 4)
         load_w1(1, 0, 4)
         for q in range(4):
-            nc.sync.dma_start(
+            nc.gpsimd.dma_start(
                 w2_scales_sb[32 * q : 32 * q + 4, :].bitcast(I32), w2_scales[0, 4 * q : 4 * q + 4, :].bitcast(I32)
             )
         load_x(1)
@@ -157,6 +160,7 @@ def tile_picked_route2_mlprelu_p_kernel(tc, x_words, x_scales, gate, w1, w2_word
         w2_words_sb = at(W1_AT[0] + 4 * S, "w2_words_sb", [P, 2 * N], U8)
         nc.sync.dma_start(w2_words_sb[:].bitcast(I32), w2_words[0].bitcast(I32))
         nc.sync.dma_start(gate_sb[:, :CHUNK], gate[:, :CHUNK])
+        nc.sync.dma_start(dst_sb[:], dst)
         nc.sync.dma_start(gate_sb[:, CHUNK:], gate[:, CHUNK:])
 
         def first_layer(c, z, opens):

@@ -70,17 +70,13 @@ def tile_picked_route2_mlprelu_p_kernel(tc, x_words, x_scales, gate, w1, w2_word
         nc.sync.dma_start(offs_sb[:], offs)
         load_w1(0, 0, 2)
 
-        x_scales_all = own("x_scales_all", [P, T], U8)
+        x_scales_all = at(X_AT[1] + BIG - T // 2, "x_scales_all", [P, T], U8)
         nc.vector.memset(x_scales_all[:].bitcast(I32), 0)
-        for q in range(2):
+        for q in range(4):
             nc.sync.dma_start(
-                x_scales_all[32 * q : 32 * q + 8, :].bitcast(I32), x_scales[:, 4 * q : 4 * q + 4, :].bitcast(I32)
+                x_scales_all[32 * q : 32 * q + 4, :].bitcast(I32), x_scales[0, 4 * q : 4 * q + 4, :].bitcast(I32)
             )
-        for z, q in ((0, 2), (1, 3), (1, 2), (0, 3)):
-            nc.sync.dma_start(
-                x_scales_all[32 * q + 4 * z : 32 * q + 4 * z + 4, :].bitcast(I32),
-                x_scales[z, 4 * q : 4 * q + 4, :].bitcast(I32),
-            )
+        nc.sync.dma_start(x_scales_all[8:24, :].bitcast(I32), x_scales[1].bitcast(I32))
 
         window = [own("window%d" % r, [P, U], F32) for r in range(2)]
         zeros_v = at(X_AT[0] - HALF_ZEROS_BYTES, "zeros_v", [P, ZEROS], F32)
@@ -111,14 +107,19 @@ def tile_picked_route2_mlprelu_p_kernel(tc, x_words, x_scales, gate, w1, w2_word
             nc.gpsimd.dma_start(
                 w2_scales_sb[32 * q : 32 * q + 4, :].bitcast(I32), w2_scales[0, 4 * q : 4 * q + 4, :].bitcast(I32)
             )
-        load_x(1)
 
         def gather(name, dtype, source, a, b):
             picked = own(name, [P, b - a], dtype)
             nc.vector.tensor_copy(picked[:], source.indirect(entries(offs_sb, a, b)))
             return picked
 
-        x_scale = gather("x_scale", U8, x_scales_all[:], 0, S)
+        x_scale = [gather("x_scale0", U8, x_scales_all[:], 0, S), own("x_scale1", [P, S], U8)]
+        nc.vector.memset(x_scale[1][:].bitcast(I32), 0)
+        for q in range(4):
+            nc.sync.dma_start(
+                x_scale[1][32 * q + 4 : 32 * q + 8, :].bitcast(I32), x_scale[0][8 + 4 * q : 12 + 4 * q, :].bitcast(I32)
+            )
+        load_x(1)
 
         w1_bf16, w1_code, w1_scale, x_word = {}, {}, {}, {}
 
@@ -171,7 +172,7 @@ def tile_picked_route2_mlprelu_p_kernel(tc, x_words, x_scales, gate, w1, w2_word
                     lhsT=w1_code[z, t // 2][:, cols].bitcast(FP8X4),
                     lhsT_scale=w1_scale[z, t // 2][:, cols],
                     rhs=x_word[z, c].bitcast(FP8X4),
-                    rhs_scale=x_scale[4 * z :, c : c + P],
+                    rhs_scale=x_scale[z][4 * z :, c : c + P],
                     start=(opens and t == 0),
                     stop=(not opens and t == PACK - 1),
                 )

@@ -254,7 +254,8 @@ def tile_picked_route2_mlprelu_p_kernel(tc, x_words, x_scales, gate, w1, w2_word
         scatter_rows_1(s1, s2)
         plain_result(c3, 5)
         scatter_rows_1(s2, s3)
-        nc.scalar.dma_start(out[P:, :], window[1][:])
+        nc.sync.dma_start(out[P:, : U // 2], window[1][:, : U // 2])
+        nc.scalar.dma_start(out[P:, U // 2 :], window[1][:, U // 2 :])
 
         nc.vector.tensor_copy(window[0][:].indirect(entries(dst_sb, c0, c2)), gated[:, 0, :c2])
         nc.vector.tensor_tensor(window[0][:].indirect(entries(dst_sb, c2, S)), plain[:], gate_sb[:, c2:], MULT)

@@ -67,8 +67,8 @@ def tile_picked_route2_mlprelu_p_kernel(tc, x_words, x_scales, gate, w1, w2_word
 
         offs_sb = lists.tile([P, S // 16], U16, name="offs_sb")
         dst_sb = lists.tile([P, S // 16], U16, name="dst_sb")
-        nc.sync.dma_start(offs_sb[:], offs)
         load_w1(0, 0, 2)
+        nc.sync.dma_start(offs_sb[:], offs)
 
         x_scales_all = at(X_AT[1] + BIG - T // 2, "x_scales_all", [P, T], U8)
         nc.vector.memset(x_scales_all[:].bitcast(I32), 0)
@@ -254,10 +254,10 @@ def tile_picked_route2_mlprelu_p_kernel(tc, x_words, x_scales, gate, w1, w2_word
         scatter_rows_1(s1, s2)
         plain_result(c3, 5)
         scatter_rows_1(s2, s3)
-        nc.sync.dma_start(out[P:, : U // 2], window[1][:, : U // 2])
-        nc.scalar.dma_start(out[P:, U // 2 :], window[1][:, U // 2 :])
+        nc.sync.dma_start(out[P::2, :], window[1][::2, :])
+        nc.scalar.dma_start(out[P + 1 :: 2, :], window[1][1::2, :])
 
         nc.vector.tensor_copy(window[0][:].indirect(entries(dst_sb, c0, c2)), gated[:, 0, :c2])
         nc.vector.tensor_tensor(window[0][:].indirect(entries(dst_sb, c2, S)), plain[:], gate_sb[:, c2:], MULT)
-        nc.sync.dma_start(out[:P, : U // 2], window[0][:, : U // 2])
-        nc.scalar.dma_start(out[:P, U // 2 :], window[0][:, U // 2 :])
+        nc.sync.dma_start(out[:P:2, :], window[0][::2, :])
+        nc.scalar.dma_start(out[1:P:2, :], window[0][1::2, :])

@@ -123,13 +123,15 @@ def tile_picked_route2_mlprelu_p_kernel(tc, x_words, x_scales, gate, w1, w2_word
 
         w1_bf16, w1_code, w1_scale, x_word = {}, {}, {}, {}
 
-        def round_w1(z, u, copy, first=0, last=PACK, lo=0, hi=P):
+        def round_w1(z, u, on_scalar, first=0, last=PACK, lo=0, hi=P):
             if (z, u) not in w1_bf16:
                 w1_bf16[z, u] = own("w1_bf16_%d%d" % (z, u), [P, 2, P, PACK], BF16)
-            copy(
-                w1_bf16[z, u][:].rearrange("p t m j -> p m t j")[:, lo:hi, :, first:last],
-                w1_raw[z, first][:].rearrange("p j (m t) -> p m t j", t=PACK)[:, lo:hi, 2 * u : 2 * u + 2, :],
-            )
+            dest = w1_bf16[z, u][:].rearrange("p t m j -> p m j t")[:, lo:hi, first:last, :]
+            source = w1_raw[z, first][:].rearrange("p j (m t) -> p m j t", t=PACK)[:, lo:hi, :, 2 * u : 2 * u + 2]
+            if on_scalar:
+                nc.scalar.copy(dest, source)
+            else:
+                nc.vector.tensor_copy(dest.rearrange("p m j t -> p m t j"), source.rearrange("p m j t -> p m t j"))
 
         def quantise_w1(z, u):
             w1_code[z, u] = own("w1_code%d%d" % (z, u), [P, 2 * P], U32)
@@ -147,13 +149,13 @@ def tile_picked_route2_mlprelu_p_kernel(tc, x_words, x_scales, gate, w1, w2_word
 
         for first in (0, 2):
             for u in range(2):
-                round_w1(0, u, nc.scalar.copy, first, first + 2)
+                round_w1(0, u, True, first, first + 2)
         gather_words(0, 0, S)
         quantise_w1(0, 0)
         quantise_w1(0, 1)
-        round_w1(1, 0, nc.scalar.copy, hi=SCALAR_ROUNDS)
-        round_w1(1, 1, nc.vector.tensor_copy)
-        round_w1(1, 0, nc.vector.tensor_copy, lo=SCALAR_ROUNDS)
+        round_w1(1, 0, True, hi=SCALAR_ROUNDS)
+        round_w1(1, 1, False)
+        round_w1(1, 0, False, lo=SCALAR_ROUNDS)
         quantise_w1(1, 1)
         quantise_w1(1, 0)
 

@@ -72,10 +72,8 @@ def tile_picked_route2_mlprelu_p_kernel(tc, x_words, x_scales, gate, w1, w2_word
 
         x_scales_all = at(X_AT[1] + BIG - T // 2, "x_scales_all", [P, T], U8)
         nc.vector.memset(x_scales_all[:].bitcast(I32), 0)
-        for q in range(4):
-            nc.sync.dma_start(
-                x_scales_all[32 * q : 32 * q + 4, :].bitcast(I32), x_scales[0, 4 * q : 4 * q + 4, :].bitcast(I32)
-            )
+        for r in range(4):
+            nc.sync.dma_start(x_scales_all[r::32, :].bitcast(I32), x_scales[0, r::4, :].bitcast(I32))
         nc.sync.dma_start(x_scales_all[8:24, :].bitcast(I32), x_scales[1].bitcast(I32))
 
         window = [own("window%d" % r, [P, U], F32) for r in range(2)]
@@ -115,10 +113,8 @@ def tile_picked_route2_mlprelu_p_kernel(tc, x_words, x_scales, gate, w1, w2_word
 
         x_scale = [gather("x_scale0", U8, x_scales_all[:], 0, S), own("x_scale1", [P, S], U8)]
         nc.vector.memset(x_scale[1][:].bitcast(I32), 0)
-        for q in range(4):
-            nc.sync.dma_start(
-                x_scale[1][32 * q + 4 : 32 * q + 8, :].bitcast(I32), x_scale[0][8 + 4 * q : 12 + 4 * q, :].bitcast(I32)
-            )
+        for r in range(4):
+            nc.sync.dma_start(x_scale[1][4 + r :: 32, :].bitcast(I32), x_scale[0][8 + r : 24 : 4, :].bitcast(I32))
         load_x(1)
 
         w1_bf16, w1_code, w1_scale, x_word = {}, {}, {}, {}

@@ -30,7 +30,6 @@ HALF_ZEROS_BYTES = 2 * ZEROS
 CHUNK = 256
 GATHERS = (0, 128, 384, 768, 1024)
 SCATTERS = (0, 256, 640, 1024)
-SCALAR_ROUNDS = 96
 VECTOR_RELU = (384, 896)
 
 
@@ -119,11 +118,11 @@ def tile_picked_route2_mlprelu_p_kernel(tc, x_words, x_scales, gate, w1, w2_word
 
         w1_bf16, w1_code, w1_scale, x_word = {}, {}, {}, {}
 
-        def round_w1(z, u, on_scalar, first=0, last=PACK, lo=0, hi=P):
+        def round_w1(z, u, on_scalar, first=0, last=PACK):
             if (z, u) not in w1_bf16:
                 w1_bf16[z, u] = own("w1_bf16_%d%d" % (z, u), [P, 2, P, PACK], BF16)
-            dest = w1_bf16[z, u][:].rearrange("p t m j -> p m j t")[:, lo:hi, first:last, :]
-            source = w1_raw[z, first][:].rearrange("p j (m t) -> p m j t", t=PACK)[:, lo:hi, :, 2 * u : 2 * u + 2]
+            dest = w1_bf16[z, u][:].rearrange("p t m j -> p m j t")[:, :, first:last, :]
+            source = w1_raw[z, first][:].rearrange("p j (m t) -> p m j t", t=PACK)[:, :, :, 2 * u : 2 * u + 2]
             if on_scalar:
                 nc.scalar.copy(dest, source)
             else:
@@ -149,9 +148,8 @@ def tile_picked_route2_mlprelu_p_kernel(tc, x_words, x_scales, gate, w1, w2_word
         gather_words(0, 0, S)
         quantise_w1(0, 0)
         quantise_w1(0, 1)
-        round_w1(1, 0, True, hi=SCALAR_ROUNDS)
+        round_w1(1, 0, True)
         round_w1(1, 1, False)
-        round_w1(1, 0, False, lo=SCALAR_ROUNDS)
         quantise_w1(1, 1)
         quantise_w1(1, 0)
 

@@ -28,9 +28,9 @@ ZEROS = 32
 HALF_ZEROS_BYTES = 2 * ZEROS
 
 CHUNK = 256
-GATHERS = (0, 128, 384, 768, 1024)
+GATHERS = (0, 128, 384, 640, 1024)
 SCATTERS = (0, 256, 640, 1024)
-VECTOR_RELU = (384, 896)
+VECTOR_RELU = (512, 896)
 
 
 def tile_picked_route2_mlprelu_p_kernel(tc, x_words, x_scales, gate, w1, w2_words, w2_scales, offs, dst, out):
@@ -174,13 +174,20 @@ def tile_picked_route2_mlprelu_p_kernel(tc, x_words, x_scales, gate, w1, w2_word
                 )
 
         acc = {c: bank("h%d" % c, c // P, [P, PACK, P]) for c in range(0, S, P)}
-        for c in range(0, S - CHUNK, P):
-            first_layer(c, 0, True)
+        for c in range(0, S, P):
+            if c not in VECTOR_RELU:
+                first_layer(c, 0, True)
 
         for a, b in zip(GATHERS, GATHERS[1:]):
             gather_words(1, a, b)
+
+        def finish_tile(c):
+            first_layer(c, 1, c in VECTOR_RELU)
+            if c in VECTOR_RELU:
+                first_layer(c, 0, False)
+
         for c in range(0, S - CHUNK, P):
-            first_layer(c, 1, False)
+            finish_tile(c)
 
         gated = own("gated", [P, 2, S], F32)
         h_bf16, h_code, h_scale = {}, {}, {}
@@ -219,20 +226,21 @@ def tile_picked_route2_mlprelu_p_kernel(tc, x_words, x_scales, gate, w1, w2_word
             nc.vector.tensor_tensor(gated[:, r, a:b], y[:], gate_sb[:, a:b], MULT)
 
         c0, c1, c2, c3 = range(0, S, CHUNK)
-        for a in (c0, c1):
-            relu(a)
-            quantise_h(a)
+        relu(c0)
+        quantise_h(c0)
+        relu(c1)
+        relu(c2)
         gated_result(1, c0, c1, 0)
         for c in range(c3, S, P):
-            first_layer(c, 1, True)
-            first_layer(c, 0, False)
-        relu(c2)
+            finish_tile(c)
+        quantise_h(c1)
         quantise_h(c2)
         relu(c3)
-        gated_result(1, c1, c3, 1)
+        gated_result(1, c1, c2, 1)
         quantise_h(c3)
-        gated_result(0, c0, c2, 2)
-        gated_result(1, c3, S, 3)
+        gated_result(1, c2, c3, 2)
+        gated_result(0, c0, c2, 3)
+        gated_result(1, c3, S, 5)
 
         plain = own("plain", [P, S - c2], F32)
 
@@ -248,7 +256,7 @@ def tile_picked_route2_mlprelu_p_kernel(tc, x_words, x_scales, gate, w1, w2_word
         scatter_rows_1(s0, s1)
         plain_result(c2, 4)
         scatter_rows_1(s1, s2)
-        plain_result(c3, 5)
+        plain_result(c3, 6)
         scatter_rows_1(s2, s3)
         nc.sync.dma_start(out[P::2, :], window[1][::2, :])
         nc.scalar.dma_start(out[P + 1 :: 2, :], window[1][1::2, :])

from contextlib import ExitStack

import concourse.mybir as mybir

F32 = mybir.dt.float32
BF16 = mybir.dt.bfloat16
I32 = mybir.dt.int32
U32 = mybir.dt.uint32
U16 = mybir.dt.uint16
U8 = mybir.dt.uint8
FP8X4 = mybir.dt.float8_e4m3fn_x4
FP4X4 = mybir.dt.float4_e2m1fn_x4
RELU = mybir.ActivationFunctionType.Relu
COPY = mybir.ActivationFunctionType.Copy
MULT = mybir.AluOpType.mult

K, T, S, H, N, U = 1024, 2048, 1024, 512, 256, 2048
P = 128
PACK = 4
K_PASS = P * PACK
BANK_BYTES = 2048
FLOPS = 2 * K * H * S + 2 * H * N * S

BIG = 8192
W1_AT = (0, 2 * BIG)
X_AT = (BIG, 3 * BIG)
ZEROS = 32
HALF_ZEROS_BYTES = 2 * ZEROS

CHUNK = 256
GATHERS = (0, 128, 384, 640, 1024)
SCATTERS = (0, 256, 640, 1024)
VECTOR_RELU = (512, 896)


def tile_picked_route2_mlprelu_p_kernel(tc, x_words, x_scales, gate, w1, w2_words, w2_scales, offs, dst, out):
    nc = tc.nc
    with ExitStack() as ctx:
        lists = ctx.enter_context(tc.tile_pool(name="lists", bufs=1))
        keep = ctx.enter_context(tc.tile_pool(name="keep", bufs=1))
        shared = ctx.enter_context(tc.tile_pool(name="shared", bufs=1))
        psum = ctx.enter_context(tc.psum_pool(name="psum", bufs=1))

        def own(name, shape, dtype):
            return keep.tile(shape, dtype, name=name, align_bytes=64)

        def at(offset, name, shape, dtype):
            return shared.tile(shape, dtype, name=name, offset=offset, align_bytes=64)

        def bank(name, index, shape):
            return psum.tile(shape, F32, name=name, offset=BANK_BYTES * index)

        def entries(list_tile, a, b):
            return list_tile[:, a // 16 : b // 16]

        w1_raw, x_all = {}, {}

        def load_w1(z, first, last):
            w1_raw[z, first] = at(W1_AT[z] + 4 * H * first, "w1_raw%d%d" % (z, first), [P, last - first, H], F32)
            rows = w1[K_PASS * z : K_PASS * (z + 1), :].rearrange("(p j) c -> p j c", j=PACK)
            nc.sync.dma_start(w1_raw[z, first][:], rows[:, first:last, :])

        def load_x(z):
            x_all[z] = at(X_AT[z], "x_all%d" % z, [P, T], I32)
            nc.sync.dma_start(x_all[z][:], x_words[z].rearrange("p c r -> p (c r)").bitcast(I32))

        offs_sb = lists.tile([P, S // 16], U16, name="offs_sb")
        dst_sb = lists.tile([P, S // 16], U16, name="dst_sb")
        load_w1(0, 0, 2)
        nc.sync.dma_start(offs_sb[:], offs)

        x_scales_all = at(X_AT[1] + BIG - T // 2, "x_scales_all", [P, T], U8)
        nc.vector.memset(x_scales_all[:].bitcast(I32), 0)
        for r in range(4):
            nc.sync.dma_start(x_scales_all[r::32, :].bitcast(I32), x_scales[0, r::4, :].bitcast(I32))
        nc.sync.dma_start(x_scales_all[8:24, :].bitcast(I32), x_scales[1].bitcast(I32))

        window = [own("window%d" % r, [P, U], F32) for r in range(2)]
        zeros_v = at(X_AT[0] - HALF_ZEROS_BYTES, "zeros_v", [P, ZEROS], F32)
        zeros_s = at(X_AT[1] - HALF_ZEROS_BYTES, "zeros_s", [P, ZEROS], F32)
        nc.vector.memset(zeros_v[:], 0.0)
        nc.vector.memset(zeros_s[:], 0.0)
        w2_scales_sb = own("w2_scales_sb", [P, N], U8)
        nc.vector.memset(w2_scales_sb[:].bitcast(I32), 0)
        nc.vector.tensor_copy(
            window[0][:, : 2 * ZEROS].rearrange("p (a b) -> p a b", b=ZEROS),
            zeros_v[:].unsqueeze(1).to_broadcast([P, 2, ZEROS]),
        )
        nc.scalar.activation(out=window[1][:, :ZEROS], in_=zeros_s[:], func=COPY)
        nc.vector.tensor_copy(
            window[0][:, 2 * ZEROS :].rearrange("p (a b) -> p a b", b=2 * ZEROS),
            window[0][:, : 2 * ZEROS].unsqueeze(1).to_broadcast([P, U // (2 * ZEROS) - 1, 2 * ZEROS]),
        )
        nc.scalar.activation(
            out=window[1][:, ZEROS:].rearrange("p (a b) -> p a b", b=ZEROS),
            in_=window[1][:, :ZEROS].unsqueeze(1).to_broadcast([P, U // ZEROS - 1, ZEROS]),
            func=COPY,
        )

        load_x(0)
        load_w1(0, 2, 4)
        load_w1(1, 0, 4)
        for q in range(4):
            nc.gpsimd.dma_start(
                w2_scales_sb[32 * q : 32 * q + 4, :].bitcast(I32), w2_scales[0, 4 * q : 4 * q + 4, :].bitcast(I32)
            )

        def gather(name, dtype, source, a, b):
            picked = own(name, [P, b - a], dtype)
            nc.vector.tensor_copy(picked[:], source.indirect(entries(offs_sb, a, b)))
            return picked

        x_scale = [gather("x_scale0", U8, x_scales_all[:], 0, S), own("x_scale1", [P, S], U8)]
        nc.vector.memset(x_scale[1][:].bitcast(I32), 0)
        for r in range(4):
            nc.sync.dma_start(x_scale[1][4 + r :: 32, :].bitcast(I32), x_scale[0][8 + r : 24 : 4, :].bitcast(I32))
        load_x(1)

        w1_bf16, w1_code, w1_scale, x_word = {}, {}, {}, {}

        def round_w1(z, u, on_scalar, first=0, last=PACK):
            if (z, u) not in w1_bf16:
                w1_bf16[z, u] = own("w1_bf16_%d%d" % (z, u), [P, 2, P, PACK], BF16)
            dest = w1_bf16[z, u][:].rearrange("p t m j -> p m j t")[:, :, first:last, :]
            source = w1_raw[z, first][:].rearrange("p j (m t) -> p m j t", t=PACK)[:, :, :, 2 * u : 2 * u + 2]
            if on_scalar:
                nc.scalar.copy(dest, source)
            else:
                nc.vector.tensor_copy(dest.rearrange("p m j t -> p m t j"), source.rearrange("p m j t -> p m t j"))

        def quantise_w1(z, u):
            w1_code[z, u] = own("w1_code%d%d" % (z, u), [P, 2 * P], U32)
            w1_scale[z, u] = own("w1_scale%d%d" % (z, u), [P, 2 * P], U8)
            nc.vector.quantize_mx(
                out=w1_code[z, u][:].bitcast(FP8X4),
                scales=w1_scale[z, u][:],
                in_=w1_bf16[z, u][:].rearrange("p t m j -> p (t m j)"),
            )

        def gather_words(z, a, b):
            picked = gather("x_word%d_%d" % (z, a), U32, x_all[z][:].bitcast(U32), a, b)
            for c in range(a, b, P):
                x_word[z, c] = picked[:, c - a : c - a + P]

        for first in (0, 2):
            for u in range(2):
                round_w1(0, u, True, first, first + 2)
        gather_words(0, 0, S)
        quantise_w1(0, 0)
        quantise_w1(0, 1)
        round_w1(1, 0, True)
        round_w1(1, 1, False)
        quantise_w1(1, 1)
        quantise_w1(1, 0)

        gate_sb = at(W1_AT[0], "gate_sb", [P, S], F32)
        w2_words_sb = at(W1_AT[0] + 4 * S, "w2_words_sb", [P, 2 * N], U8)
        nc.sync.dma_start(w2_words_sb[:].bitcast(I32), w2_words[0].bitcast(I32))
        nc.sync.dma_start(gate_sb[:, :CHUNK], gate[:, :CHUNK])
        nc.sync.dma_start(dst_sb[:], dst)
        nc.sync.dma_start(gate_sb[:, CHUNK:], gate[:, CHUNK:])

        def first_layer(c, z, opens):
            for t in range(PACK):
                cols = slice((t % 2) * P, (t % 2 + 1) * P)
                nc.tensor.matmul_mx(
                    out=acc[c][:, t, :],
                    lhsT=w1_code[z, t // 2][:, cols].bitcast(FP8X4),
                    lhsT_scale=w1_scale[z, t // 2][:, cols],
                    rhs=x_word[z, c].bitcast(FP8X4),
                    rhs_scale=x_scale[z][4 * z :, c : c + P],
                    start=(opens and t == 0),
                    stop=(not opens and t == PACK - 1),
                )

        acc = {c: bank("h%d" % c, c // P, [P, PACK, P]) for c in range(0, S, P)}
        for c in range(0, S, P):
            if c not in VECTOR_RELU:
                first_layer(c, 0, True)

        for a, b in zip(GATHERS, GATHERS[1:]):
            gather_words(1, a, b)

        def finish_tile(c):
            first_layer(c, 1, c in VECTOR_RELU)
            if c in VECTOR_RELU:
                first_layer(c, 0, False)

        for c in range(0, S - CHUNK, P):
            finish_tile(c)

        gated = own("gated", [P, 2, S], F32)
        h_bf16, h_code, h_scale = {}, {}, {}

        def relu(a):
            h_bf16[a] = own("h_bf16_%d" % a, [P, CHUNK, PACK], BF16)
            for c in range(a, a + CHUNK, P):
                dest, sums = h_bf16[a][:, c - a : c - a + P, :], acc[c][:].rearrange("p t n -> p n t")
                if c in VECTOR_RELU:
                    nc.vector.tensor_scalar_max(dest, sums, 0.0)
                else:
                    nc.scalar.activation(out=dest, in_=sums, func=RELU)

        def quantise_h(a):
            h_code[a] = own("h_code%d" % a, [P, CHUNK], U32)
            h_scale[a] = own("h_scale%d" % a, [P, CHUNK], U8)
            nc.vector.quantize_mx(
                out=h_code[a][:].bitcast(FP8X4), scales=h_scale[a][:], in_=h_bf16[a][:].rearrange("p n t -> p (n t)")
            )

        def second_layer(y, r, a):
            nc.tensor.matmul_mx(
                out=y,
                lhsT=w2_words_sb[:, 2 * P * r : 2 * P * (r + 1)].bitcast(FP4X4),
                lhsT_scale=w2_scales_sb[:, P * r : P * (r + 1)],
                rhs=h_code[a][:].bitcast(FP8X4),
                rhs_scale=h_scale[a][:],
                start=True,
                stop=True,
            )

        def gated_result(r, a, b, bank_index):
            y = bank("y%d_%d" % (r, a), bank_index, [P, b - a])
            for c in range(a, b, CHUNK):
                second_layer(y[:, c - a : c - a + CHUNK], r, c)
            nc.vector.tensor_tensor(gated[:, r, a:b], y[:], gate_sb[:, a:b], MULT)

        c0, c1, c2, c3 = range(0, S, CHUNK)
        relu(c0)
        quantise_h(c0)
        relu(c1)
        relu(c2)
        gated_result(1, c0, c1, 0)
        for c in range(c3, S, P):
            finish_tile(c)
        quantise_h(c1)
        quantise_h(c2)
        relu(c3)
        gated_result(1, c1, c2, 1)
        quantise_h(c3)
        gated_result(1, c2, c3, 2)
        gated_result(0, c0, c2, 3)
        gated_result(1, c3, S, 5)

        plain = own("plain", [P, S - c2], F32)

        def scatter_rows_1(a, b):
            nc.scalar.activation(out=window[1][:].indirect(entries(dst_sb, a, b)), in_=gated[:, 1, a:b], func=COPY)

        def plain_result(a, bank_index):
            y = bank("y0_%d" % a, bank_index, [P, CHUNK])
            second_layer(y[:], 0, a)
            nc.scalar.copy(plain[:, a - c2 : a - c2 + CHUNK], y[:])

        s0, s1, s2, s3 = SCATTERS
        scatter_rows_1(s0, s1)
        plain_result(c2, 4)
        scatter_rows_1(s1, s2)
        plain_result(c3, 6)
        scatter_rows_1(s2, s3)
        nc.sync.dma_start(out[P::2, :], window[1][::2, :])
        nc.scalar.dma_start(out[P + 1 :: 2, :], window[1][1::2, :])

        nc.vector.tensor_copy(window[0][:].indirect(entries(dst_sb, c0, c2)), gated[:, 0, :c2])
        nc.vector.tensor_tensor(window[0][:].indirect(entries(dst_sb, c2, S)), plain[:], gate_sb[:, c2:], MULT)
        nc.sync.dma_start(out[:P:2, :], window[0][::2, :])
        nc.scalar.dma_start(out[1:P:2, :], window[0][1::2, :])
